import numpy as np, ml_dtypes
CORES = [3,7,11,15,131,135,139,143]
N = 8
BF = ml_dtypes.bfloat16
L, S, Q = 128, 4, 512
def packed(rng, st):
    fr = np.diff(np.append(st, 2048)); sy = rng.permutation(256)[:len(st)]
    return np.stack([np.repeat(2048 * (fr - 1) + st, fr), np.repeat(sy, fr)])
def model(rng, n):
    return packed(rng, np.concatenate([[0], np.sort(rng.integers(0, 2048 - 8 * n + 1, n - 1)) + 8 * np.arange(1, n)]).astype(np.int64))
def both(m):
    return {"models": np.ascontiguousarray(m[:, :, 0]).astype(np.int32), "letters": np.ascontiguousarray(m[:, :, 1]).astype(np.int32)}
def models_of(rng, n):
    return both(np.stack([np.stack([model(rng, int(n[r, g])) for g in range(8)]) for r in range(N)]))
def some_states(rng):
    return np.clip(np.exp2(12 + 8 * rng.random((N, 8, L))), 4096, 1048575).astype(np.int32)
def some_bytes(rng):
    return rng.integers(0, 256, (N, 8, Q)).astype(np.int32)
def same(p):
    return np.repeat(p[None], N, axis=0).astype(np.int32)
def some_places(rng):
    return same(np.stack([rng.permutation(N * Q) for g in range(8)]))
def setup_inputs(rng):
    n = np.exp2(1 + 6.5 * rng.random((N, 8))).astype(np.int64); n[:, rng.integers(0, 8)] = 256
    m = models_of(rng, n)
    return {"states": some_states(rng), "models": m["models"], "letters": m["letters"], "stock": some_bytes(rng), "places": some_places(rng)}
def setup_inputs_every(rng):
    x = some_states(rng); x[:, :, 0] = 4096; x[:, :, L - 1] = 1048575
    m = models_of(rng, np.full((N, 8), 256)); p = some_places(rng); g = rng.permutation(8)
    p[:, g[0]] = np.arange(N * Q); p[:, g[1]] = np.arange(N * Q)[::-1]
    return {"states": x, "models": m["models"], "letters": m["letters"], "stock": some_bytes(rng), "places": p}
def setup_inputs_dry(rng):
    d = setup_inputs(rng); n = np.exp2(1 + 6.5 * rng.random((N, 8))).astype(np.int64); g = rng.permutation(8); p = rng.permutation(N)
    n[:, g[:3]] = 1
    for i in range(5):
        n[p[i % N], g[3 + i]] = 1
    d.update(models_of(rng, n)); return d
def setup_inputs_edge(rng):
    k = 2 ** rng.integers(4, 11, (N, 8, 1)); up = 4096 // k; a = rng.integers(0, 2048, (N, 8, L)) // k * k
    kind = rng.integers(0, 4, (N, 8, L)); kind[:, :, :4] = np.arange(4)
    x = np.where(kind == 0, 2048 * up + a, np.where(kind == 1, 2048 * (up - 1) + a + k - 1, np.where(kind == 2, 4096, 1048575)))
    m = both(np.stack([np.stack([packed(rng, np.arange(0, 2048, int(k[r, g, 0]))) for g in range(8)]) for r in range(N)]))
    return {"states": x.astype(np.int32), "models": m["models"], "letters": m["letters"], "stock": (255 * rng.integers(0, 2, (N, 8, Q))).astype(np.int32), "places": some_places(rng)}
def setup_inputs_few(rng):
    x = rng.integers(2 ** 19, 2 ** 20, (N, 8, L)); x[:, :, 0] = rng.integers(4096, 8192, (N, 8)); x[:, :, L - 1] = rng.integers(4096, 8192, (N, 8)); x[:, :, 1] = rng.integers(8192, 16384, (N, 8))
    p = rng.permutation(N); m = both(np.stack([np.stack([packed(rng, np.arange(0, 2048, 8 if p[g % N] == r else 1024)) for g in range(8)]) for r in range(N)]))
    return {"states": x.astype(np.int32), "models": m["models"], "letters": m["letters"], "stock": some_bytes(rng), "places": some_places(rng)}
def setup_inputs_spread(rng):
    slot = np.arange(2048); e = np.floor((slot + 1) * rng.random((N, 8, 2048)) ** 3).astype(np.int64); e = np.minimum(e, slot)
    lo = np.maximum(e, 7); w = np.minimum(lo + np.floor((2048 - lo) * rng.random((N, 8, 2048)) ** 4).astype(np.int64), 2047)
    m = 2048 * w + slot - e
    b = np.minimum(np.floor(256 * rng.random((N, 8, Q)) ** 6), 255)
    return {"states": some_states(rng), "models": m.astype(np.int32), "letters": rng.integers(0, 256, (N, 8, 2048)).astype(np.int32), "stock": b.astype(np.int32), "places": some_places(rng)}
def check_inputs(d):
    x, t, a, b, p = d["states"], d["models"].astype(np.int64), d["letters"], d["stock"], d["places"]; bad = []; slot = np.arange(2048)
    if not ((x >= 4096) & (x < 1048576)).all(): bad.append("states")
    if not ((t >= 14336) & (t < 4194304) & ((t & 2047) <= slot) & (slot <= (t & 2047) + (t >> 11))).all(): bad.append("models")
    if not ((a >= 0) & (a < 256)).all(): bad.append("letters")
    if not ((b >= 0) & (b < 256)).all(): bad.append("stock")
    if not ((np.sort(p, axis=2) == np.arange(N * Q)).all() and (p == p[:1]).all()): bad.append("places")
    return bad
def whole(b):
    return np.ascontiguousarray(b.transpose(1, 2, 0)).reshape(8, -1)
def line(v, s):
    return np.ascontiguousarray(v.transpose(1, 0, 2)).reshape(8, -1)
def unline(u, s):
    return u.reshape(8, N, L).transpose(1, 0, 2)
def reference(states, models, letters, stock, places):
    x = states.astype(np.int64); t = models.astype(np.int64); pool = whole(stock.astype(np.int64)); seq = places[0].astype(np.int64)
    syms = np.zeros((N, 8, S * L), np.int32); used = np.zeros(8, np.int64)
    for s in range(S):
        slot = x & 2047; e = np.take_along_axis(t, slot, 2)
        syms[:, :, s * L:(s + 1) * L] = np.take_along_axis(letters, slot, 2)
        x = ((e >> 11) + 1) * (x >> 11) + slot - (e & 2047)
        reads = x < 4096; w = line(reads, s).astype(np.int64)
        at = used[:, None] + np.add.accumulate(w, axis=1) - w
        x = np.where(reads, 256 * x + unline(np.take_along_axis(pool, np.take_along_axis(seq, at, 1), 1), s), x)
        used = used + np.add.reduce(w, axis=1)
    return {"syms": np.asarray(syms, np.float32), "last": np.asarray(x, np.float32)}

@@ -1,0 +1,433 @@
+from concourse.bass import DstId, RemoteDMATransfer
+from concourse.mybir import AluOpType as A, ActivationFunctionType as F
+
+I32, U16, F32, B16 = "int32", "uint16", "float32", "bfloat16"
+SCRATCH = {}
+for _i, _w, _t in ((0, 8, I32), (1, 16, I32), (2, 16, B16), (3, 16, B16), (4, 4, F32), (5, 1, F32)):
+    SCRATCH["snd%d" % _i] = SCRATCH["land%d" % _i] = ("dram", [8, 128, _w], _t)
+for _t, _l in (
+        (I32, "ic 128 ij 128 is1 128 ip 8 i2 8 i1 8 i4 4 i3o 32 cq 8 c7 8 c3 8 ch 8 c1 8 c8 8 sgi 128 i32i 32"
+              " ind4i 4 pl 32 zz 32 zh 32 loi 32 lh 32 poolw 256 wq 128 win 2048 lti 128 c0 8 k 8 lo 8 f3 8 h2 8"
+              " y 8 ylo 8 sl 8 mt 128 mf 128 mc 128 mq 128 sa 128"),
+        (U16, "permo 8 clist 8 offm 32 off 32 off0 8 off2 32"),
+        (F32, "qf 8 qs 8 p15 8 c16 8 pcf 8 maskf 128 blkf 128 bmask 128 hxm 128 sgf 128 i32f 32 ind4 4 lz 256 selx 128 g0 128"
+              " gm 128 sc 128 slm 8 u 8 u4 8 pr 8 xq 8 g256 8 xl 8 lg 512 outs 512 sp 128 mff 128 mn 128 mr 128 mv 128"),
+        (B16, "blkb 128 lt 128 e8 128 ones 128 c255 128 n255 128 idn 128 nid 128 i128 8 selw 1024 sgb 128 km 128 zer 128"
+              " lob 32 selm 512 gby 512 bw 4112 ltb 128 lw 2048 thw 2048 qb 128 maskb 128 w 8 wm 128 pp 8 ppx 432 sb 128"
+              " gb 128")):
+    _l = _l.split()
+    for _i in range(0, len(_l), 2):
+        SCRATCH[_l[_i]] = ("sbuf", [128, int(_l[_i + 1])], _t)
+SCRATCH["lor"] = ("sbuf", [8, 512], B16)
+for _i in ("ps0", "ps1", "ps2", "ps3", "ps4", "psr", "psz", "psb"):
+    SCRATCH[_i] = ("psum", [128, 512], F32)
+SEMAPHORES = ["gi", "v", "t", "s", "ls", "a0", "a1", "a2", "a3", "a4", "a5",
+              "l0", "l1", "own0", "own1", "lmt", "lpl", "lzz", "llt", "dlo", "dth", "dlt", "dow2", "dow3", "dst", "dpa",
+              "dpb", "dwa", "dw", "dtw", "dlw", "dsy", "dow4", "dla", "dow5", "fsy", "fla"]
+
+
+def rank_program(g, core, T, topo):
+    me = T.rank_of(core)
+    if me is None:
+        return
+    Q = {"g": g, "v": g.vector, "s": g.scalar, "y": g.sync, "t": g.tensor}
+    cnt, seen, waited = {}, {}, {}
+
+    def did(ins, sem, n=1):
+        ins.then_inc(T.sem[sem], n)
+        cnt[sem] = cnt.get(sem, 0) + n
+        return (sem, cnt[sem])
+
+    def need(q, *toks):
+        for sem, val in toks:
+            if seen.get((q, sem), 0) < val:
+                Q[q].wait_ge(T.sem[sem], val)
+                seen[(q, sem)] = val
+                waited[sem] = max(waited.get(sem, 0), val)
+
+    v, ac, te = g.vector, g.scalar, g.tensor
+
+    def dma(q, out, in_, sem, *toks):
+        need(q, *toks)
+        return did(Q[q].dma_start(out, in_), sem, 16)
+
+    def V(ins):
+        return did(ins, "v")
+
+    def S(ins):
+        return did(ins, "s")
+
+    def P(ins):
+        return did(ins, "t")
+
+    def ts(out, in_, s1, s2, o1, *o2):
+        return V(v.tensor_scalar(out, in_, s1, s2, o1, *o2))
+
+    def tt(out, a, b, op):
+        return V(v.tensor_tensor(out, a, b, op))
+
+    def scan(out, a, b, o1, o2):
+        return V(v.tensor_tensor_scan(out, a, b, 0.0, o1, o2))
+
+    def copy(out, in_):
+        return V(v.tensor_copy(out, in_))
+
+    def fill(ap, x):
+        return V(v.memset(ap, x))
+
+    def act(out, in_, *sc):
+        return S(ac.activation(out, in_, F.Copy, *sc))
+
+    others = [d for d in T.cores if d != core]
+    near = topo.cores_of(core)
+    eng, k, kk = {}, 0, 0
+    for d in others:
+        es = topo.engines(core, d)
+        if d in near:
+            kk += 1
+            eng[d] = es[-kk]
+        else:
+            eng[d] = (es[0::2] + es[1::2])[k]
+            k += 1
+
+    def send(src, dst, arr):
+        tr = []
+        for d in others:
+            rid, pnc = topo.addr(d, core)
+            tr.append(RemoteDMATransfer(dst_ids=[DstId(rid=rid, pnc=pnc)], dma_engine_mask=1 << eng[d],
+                                        remote_sem=T.sem[arr], src=src[T.rank_of(d)], dst=dst[me]))
+        g.remote_dma_fused(tr, local_sem=T.sem.ls)
+        cnt["ls"] = cnt.get("ls", 0) + len(tr)
+        cnt[arr] = len(others)
+        return (arr, len(others))
+
+    dma("s", T.snd0[:, 0:16, :], T.states[:, :], "l0")
+    dma("y", T.snd0[:, 16:80, :], T.stock[:, :], "l0")
+    l0 = dma("s", T.snd0[:, 80:128, :], T.models[:, 0:384], "l0")
+    l1 = dma("y", T.snd1[:, :, :], T.models[:, :], "l1")
+    lmt = dma("y", T.mt[:, :], T.models[:, :], "lmt")
+    lpl = dma("y", T.pl[:, :], T.places[me, :], "lpl")
+    for s in range(4):
+        for h in range(2):
+            t = 1024 * s + 512 * h
+            lzz = dma("s", T.zz[32 * s:32 * s + 32, 16 * h:16 * h + 16], T.places[me, t:t + 512], "lzz")
+    llt = dma("y", T.lti[:, :], T.letters[:, :], "llt")
+    dma("y", T.land0[me, 0:16, :], T.states[me, :], "own0")
+    own0 = dma("y", T.land0[me, 16:80, :], T.stock[me, :], "own0")
+    own1 = dma("y", T.land1[me, :, :], T.models[me, :], "own1")
+
+    def pattern(out, pat, base, mul):
+        return did(g.iota(out, pat, base, mul), "gi")
+
+    def choose(out, in_, step, op, mul, *toks):
+        need("g", *toks)
+        return did(g.affine_select(out, in_, [[step, 128]], op, 0.0, 0, mul), "gi")
+
+    ip = pattern(T.ip[:, 0:1], [[0, 1]], 0, 1)
+    ic = pattern(T.ic[:, :], [[-16, 8], [0, 16]], 0, 1)
+    is1 = pattern(T.is1[:, :], [[1, 128]], 0, 128)
+    ij = pattern(T.ij[:, :], [[0, 8], [1, 16]], 0, 0)
+    need("g", l0)
+    a0 = send(T.snd0, T.land0, "a0")
+    need("g", l1)
+    a1 = send(T.snd1, T.land1, "a1")
+    i4 = pattern(T.i4[:, :], [[-8, 4]], 0, 1)
+    i3o = pattern(T.i3o[:, :], [[-32, 4], [-1, 8]], 128, 1)
+    i1 = pattern(T.i1[:, :], [[1, 8]], 0, 0)
+    i2 = pattern(T.i2[:, :], [[2, 8]], 0, 0)
+
+    ones = fill(T.ones[:, :], 1.0)
+    fill(T.c255[:, :], 255.0)
+    n255 = fill(T.n255[:, :], -255.0)
+    lt = choose(T.lt[:, :], T.ones[:, :], 1, A.is_gt, -1, ones)
+    lz0 = fill(T.lz[:, :], 0.0)
+    need("v", ip)
+    cq = ts(T.cq[:, 0:1], T.ip[:, 0:1], 15, None, A.bitwise_and)
+    p15 = ts(T.p15[:, 0:1], T.ip[:, 0:1], 15.0, None, A.mult)
+    ch = ts(T.ch[:, 0:1], T.ip[:, 0:1], 1, 7, A.arith_shift_right, A.bitwise_and)
+    c1 = ts(T.c1[:, 0:1], T.ip[:, 0:1], 1, None, A.bitwise_and)
+    need("v", ic, p15)
+    sgi = ts(T.sgi[:, :], T.ic[:, :], 4, None, A.arith_shift_right)
+    e8 = ts(T.e8[:, :], T.ic[:, :], T.p15[:, 0:1], 0.0, A.add, A.is_equal)
+    need("v", c1)
+    c8 = ts(T.c8[:, 0:1], T.c1[:, 0:1], 8.0, None, A.mult)
+    need("v", sgi)
+    sg = ts(T.sgf[:, :], T.sgi[:, :], 0.0, None, A.is_equal)
+    need("v", is1)
+    sa = ts(T.sa[:, :], T.is1[:, :], 2047, None, A.bitwise_and)
+    need("v", cq)
+    qf = copy(T.qf[:, 0:1], T.cq[:, 0:1])
+    need("v", ch, c8)
+    qs = tt(T.qs[:, 0:1], T.ch[:, 0:1], T.c8[:, 0:1], A.add)
+    need("v", sa)
+    sp = ts(T.sp[:, :], T.sa[:, :], -4095.5, None, A.add)
+    need("v", ij, qf)
+    mf = ts(T.maskf[:, :], T.ij[:, :], T.qf[:, 0:1], None, A.is_equal)
+    bf = ts(T.blkf[:, :], T.ij[:, :], 0.0, None, A.is_gt)
+    need("v", lmt)
+    mf_ = ts(T.mf[:, :], T.mt[:, :], 2.0 ** -11, 0.500244140625, A.mult, A.add)
+    mc = ts(T.mc[:, :], T.mt[:, :], 2047, None, A.bitwise_and)
+    need("v", lpl)
+    loi = ts(T.loi[:, :], T.pl[:, :], 7, None, A.bitwise_and)
+    lh = ts(T.lh[:, :], T.pl[:, :], 8, 8, A.arith_shift_right, A.bitwise_and)
+    need("v", mf_)
+    mff = copy(T.mff[:, :], T.mf[:, :])
+    need("v", mc, sp)
+    mn = tt(T.mn[:, :], T.mc[:, :], T.sp[:, :], A.subtract)
+    need("v", loi, lh)
+    lob = tt(T.lob[:, :], T.loi[:, :], T.lh[:, :], A.add)
+    need("v", mff)
+    mr = V(v.reciprocal(T.mr[:, :], T.mff[:, :]))
+    need("v", mn, mr)
+    mv = tt(T.mv[:, :], T.mn[:, :], T.mr[:, :], A.mult)
+    need("v", lzz)
+    zh = ts(T.zh[:, :], T.zz[:, :], 3, 255, A.arith_shift_right, A.bitwise_and)
+    need("v", mv)
+    mq = ts(T.mq[:, :], T.mv[:, :], -256.5, None, A.add)
+    need("v", i4, i3o)
+    n4i = ts(T.ind4i[:, :], T.i4[:, :], 31, 3, A.bitwise_and, A.arith_shift_right)
+    i3i = ts(T.i32i[:, :], T.i3o[:, :], 231, None, A.bitwise_and)
+    need("v", mq)
+    qb = copy(T.qb[:, :], T.mq[:, :])
+    need("v", n4i, i3i)
+    n4 = ts(T.ind4[:, :], T.ind4i[:, :], 0.0, None, A.is_equal)
+    i3 = ts(T.i32f[:, :], T.i32i[:, :], 128.0, None, A.is_equal)
+    need("v", n4, zh, lz0)
+    lz = None
+    for b in range(8):
+        h, bb = b // 4, b % 4
+        c = 128 * h + 16 * b
+        lz = ts(T.lz[:, c:c + 16], T.zh[:, 16 * h:16 * h + 16], T.ind4[:, bb:bb + 1], None, A.mult)
+    need("v", i1)
+    clist = copy(T.clist[:, :], T.i1[:, :])
+    need("v", llt)
+    ltb = copy(T.ltb[:, :], T.lti[:, :])
+    i128 = fill(T.i128[:, :], 1.0 / 128)
+
+    for s in range(4):
+        dlo = dma("y", T.lor[:, 128 * s:128 * s + 128], T.lob[32 * s:32 * s + 32, :], "dlo", lob)
+    need("t", dlo, e8)
+    plo = P(te.matmul(T.ps4[:, :], T.e8[0:8, :], T.lor[:, :], True, True))
+    need("t", lz, i3)
+    te.matmul(T.psz[:, 0:32], T.lz[:, 0:128], T.i32f[:, :], True, False)
+    pz = P(te.matmul(T.psz[:, 0:32], T.lz[:, 128:256], T.i32f[:, :], False, True))
+    need("v", plo, qs)
+    selm = ts(T.selm[:, :], T.ps4[:, :], T.qs[:, 0:1], None, A.is_equal)
+
+    dth = dma("y", T.snd2[:, :, :], T.qb[:, :], "dth", qb)
+    dow2 = dma("y", T.land2[me, :, :], T.qb[16 * me:16 * me + 16, :], "dow2")
+    need("g", dth)
+    a2 = send(T.snd2, T.land2, "a2")
+    choose(T.idn[:, :], T.c255[:, :], -1, A.is_equal, 1, n255)
+    nid = choose(T.nid[:, :], T.n255[:, :], -1, A.is_equal, 1)
+
+    need("s", ones, sg)
+    for b in range(8):
+        act(T.selw[:, 128 * b:128 * b + 128], T.ones[:, :], 0.0, T.sgf[:, 16 * b:16 * b + 1])
+    se = act(T.sgb[:, :], T.sgf[:, :])
+    need("s", se)
+    act(T.lw[:, 0:1024], T.selw[:, :])
+
+    need("s", a0, own0)
+    dst = dma("y", T.c0[:, :], T.land0[:, 0:16, :], "dst", a0, own0)
+    for b in range(4):
+        dpb = dma("s", T.poolw[16 * b:16 * b + 16, :], T.land0[:, 16:80, :], "dpb")
+        dpa = dma("y", T.poolw[16 * b + 64:16 * b + 80, :], T.land0[:, 16:80, :], "dpa")
+    dwa = dma("y", T.wq[:, :], T.land1[:, :, :], "dwa", a1, own1)
+    for q in range(16):
+        dw = dma("y", T.win[q:128:16, :], T.land1[:, :, :], "dw")
+    need("s", mf, bf)
+    mb = act(T.maskb[:, :], T.maskf[:, :])
+    bb = act(T.blkb[:, :], T.blkf[:, :])
+    dlt = dma("s", T.snd3[:, :, :], T.ltb[:, :], "dlt", ltb)
+    dow3 = dma("s", T.land3[me, :, :], T.ltb[16 * me:16 * me + 16, :], "dow3")
+    need("g", dlt)
+    a3 = send(T.snd3, T.land3, "a3")
+    lwf = act(T.lw[:, 1024:2048], T.selw[:, :])
+
+    need("v", dst)
+    kt = ts(T.k[:, :], T.c0[:, :], 7, 15, A.arith_shift_right, A.bitwise_and)
+    lo = ts(T.lo[:, :], T.c0[:, :], 127, None, A.bitwise_and)
+    sl = ts(T.sl[:, :], T.c0[:, :], 2047, None, A.bitwise_and)
+    need("v", kt, mf, clist)
+    km = tt(T.km[:, :], T.k[:, :].indirect(T.clist[:, :]), T.maskf[:, :], A.mult)
+    need("t", km, se)
+    pk = P(te.matmul(T.psb[:, 0:128], T.sgb[:, :], T.km[:, :], True, True))
+    need("v", lo)
+    off0 = copy(T.off0[:, :], T.lo[:, :])
+    h2 = ts(T.h2[:, :], T.c0[:, :], 2.0 ** -11, 2047.500244140625, A.mult, A.add)
+    need("v", pz)
+    offm = copy(T.offm[:, :], T.psz[:, 0:32])
+
+    gby, segc, offs, ends = {}, {}, {}, {}
+
+    def gather(s0, s1):
+        r = tt(T.gby[:, 128 * s0:128 * s1], T.poolw[:, :].indirect(T.offm[:, 8 * s0:8 * s1]),
+               T.selm[:, 128 * s0:128 * s1], A.mult)
+        for s in range(s0, s1):
+            gby[s] = r
+
+    def segment(i):
+        ps = T["ps%d" % (i % 5)]
+        s, p = i // 2, None
+        need("t", gby[s], se)
+        if i >= 5:
+            need("t", segc[i - 5])
+        for k in range(4):
+            b = 4 * (i % 2) + k
+            p = P(te.matmul(ps[:, 128 * k:128 * k + 128], T.selw[:, 128 * b:128 * b + 128],
+                            T.gby[:, 128 * s:128 * s + 128], True, True))
+        need("s", p)
+        segc[i] = act(T.bw[:, 1 + 512 * i:513 + 512 * i], ps[:, :])
+
+    def letters(s):
+        need("s", offs[s], dlw, permo)
+        lg = T.lg[:, 128 * s:128 * s + 128]
+        need("s", act(lg, T.lw[:, :].indirect(T.off[:, 8 * s:8 * s + 8])))
+        return act(T.outs[:, 128 * s:128 * s + 128], lg.indirect(T.permo[:, :]))
+
+    prev, py = None, None
+    for s in range(4):
+        c, x = 8 * s, 144 * (s - 1)
+        E = T.sc[:, 15:128:16]
+        need("v", sl)
+        offs[s] = copy(T.off[:, c:c + 8], T.sl[:, :])
+        slm = ts(T.slm[:, :], T.sl[:, :], -2048.0, None, A.add)
+        if s > 0:
+            need("t", prev, ones)
+            for j in range(s):
+                te.matmul(T.psb[:, 0:1], T.ones[:, :], ends[j], j == 0, False)
+        if s == 0:
+            need("v", pk)
+            selx = ts(T.selx[:, :], T.psb[:, 0:128], T.qf[:, 0:1], None, A.is_equal)
+            need("v", off0, selx, dwa)
+            t = tt(T.g0[:, :], T.wq[:, :].indirect(T.off0[:, :]), T.selx[:, :], A.mult)
+            need("t", t, sg)
+            t = P(te.matmul(T.psr[:, 0:128], T.sgf[:, :], T.g0[:, :], True, True))
+            need("v", dpa, dpb, offm, selm)
+            gather(0, 1)
+            segment(0)
+            segment(1)
+            gather(1, 3)
+            need("v", t, mf)
+            py = gm = tt(T.gm[:, :], T.psr[:, 0:128], T.maskf[:, :], A.mult)
+            zer = fill(T.zer[:, :], 0.0)
+            need("v", gm, bf)
+            e = scan(T.sc[:, :], T.blkf[:, :], T.gm[:, :], A.mult, A.add)
+            bm = ts(T.bmask[:, :], T.maskf[:, :], -6400.0, 4096.0, A.mult, A.add)
+            zp = fill(T.ppx[:, 15:432:144], 0.0)
+            need("v", e)
+            f3 = ts(T.f3[:, :], E, 2.0 ** -11, 0.500244140625, A.mult, A.add)
+            need("v", slm)
+            u = tt(T.u[:, :], T.slm[:, :], E, A.subtract)
+            c7 = ts(T.c7[:, 0:1], T.ip[:, 0:1], 7, None, A.bitwise_and)
+            need("v", f3, h2)
+            pr = tt(T.pr[:, :], T.f3[:, :], T.h2[:, :], A.mult)
+            need("v", u)
+            u4 = ts(T.u4[:, :], T.u[:, :], -1.0, 4096.0, A.mult, A.add)
+            con = fill(T.bw[:, 0:1], 0.0)
+            need("v", pr, u4)
+            w = tt(T.w[:, :], T.pr[:, :], T.u4[:, :], A.is_lt)
+            xq = tt(T.xq[:, :], T.pr[:, :], T.u[:, :], A.add)
+            need("v", w, zer)
+            ppc, ends[s] = T.pp[:, :], T.pp[:, 7:8]
+            pp = scan(ppc, T.w[:, :], T.zer[:, 0:8], A.add, A.max)
+            g256 = ts(T.g256[:, :], T.w[:, :], 255.0, 1.0, A.mult, A.add)
+            need("v", clist, mb)
+            wm = tt(T.wm[:, :], T.w[:, :].indirect(T.clist[:, :]), T.maskb[:, :], A.mult)
+        else:
+            need("v", offs[s], hx, dw)
+            gm = tt(T.gm[:, :], T.win[:, :].indirect(T.off[:, c:c + 8]), T.maskf[:, :], A.mult)
+            need("v", dtw)
+            wm = tt(T.wm[:, :], T.thw[:, :].indirect(T.off[:, c:c + 8]), T.hxm[:, :], A.is_ge)
+            need("v", gm)
+            e = scan(T.sc[:, :], T.blkf[:, :], T.gm[:, :], A.mult, A.add)
+            need("v", wm)
+            pp = scan(T.ppx[:, x + 16:x + 144], T.wm[:, :], T.zer[:, :], A.add, A.max)
+            ppc, ends[s] = T.ppx[:, x + 31:x + 144:16], T.ppx[:, x + 143:x + 144]
+            need("v", e)
+            f3 = ts(T.f3[:, :], E, 2.0 ** -11, 0.500244140625, A.mult, A.add)
+            need("v", slm)
+            u = tt(T.u[:, :], T.slm[:, :], E, A.subtract)
+            need("v", f3, h2)
+            pr = tt(T.pr[:, :], T.f3[:, :], T.h2[:, :], A.mult)
+        need("t", pp, lt)
+        base = P(te.matmul(T.psb[:, 0:1], T.lt[:, :], ends[s], s == 0, True))
+        if s == 0:
+            segment(2)
+            segment(3)
+            need("v", xq, g256)
+            y = tt(T.y[:, :], T.xq[:, :], T.g256[:, :], A.mult)
+        else:
+            need("t", i128, nid, zp, py)
+            te.matmul(T.psr[:, 0:8], T.idn[:, :], ppc, True, False)
+            te.matmul(T.psr[:, 0:8], T.nid[:, :], T.ppx[:, x + 15:x + 128:16], False, False)
+            pg = P(te.matmul(T.psr[:, 0:8], T.ones[:, :], T.i128[:, :], False, True))
+        need("v", base, con)
+        prev = ts(T.off2[:, c:c + 8], ppc, T.psb[:, 0:1], None, A.add)
+        if s > 0:
+            need("v", pr, u)
+            xq = tt(T.xq[:, :], T.pr[:, :], T.u[:, :], A.add)
+        else:
+            need("v", y)
+            h2 = ts(T.h2[:, :], T.y[:, :], 2.0 ** -11, 2047.500244140625, A.mult, A.add)
+            y2 = ts(T.ylo[:, :], T.y[:, :], 2047, None, A.bitwise_and)
+        need("v", prev, wm, segc[2 * s + 1])
+        t = tt(T.gb[:, :], T.bw[:, 0:1025 + 1024 * s].indirect(T.off2[:, c:c + 8]), T.wm[:, :], A.mult)
+        if s > 0:
+            need("v", xq, pg)
+            py = y = tt(T.y[:, :], T.xq[:, :], T.psr[:, 0:8], A.mult)
+        if s == 1:
+            need("v", i2, pcf)
+            permo = ts(T.permo[:, :], T.i2[:, :], T.pcf[:, 0:1], None, A.add)
+        if s == 0:
+            gather(3, 4)
+            c3 = ts(T.c3[:, 0:1], T.ip[:, 0:1], 3, 1, A.arith_shift_right, A.bitwise_and)
+        need("v", t, bb)
+        t = scan(T.sb[:, :], T.blkb[:, :], T.gb[:, :], A.mult, A.add)
+        if s == 3:
+            need("v", t, y)
+            xl = tt(T.xl[:, :], T.y[:, :], T.sb[:, 15:128:16], A.add)
+            break
+        if s > 0:
+            need("v", y)
+            y2 = ts(T.ylo[:, :], T.y[:, :], 2047, None, A.bitwise_and)
+            h2 = ts(T.h2[:, :], T.y[:, :], 2.0 ** -11, 2047.500244140625, A.mult, A.add)
+        else:
+            need("v", c7)
+            c16 = ts(T.c16[:, 0:1], T.c7[:, 0:1], 16.0, None, A.mult)
+        need("v", t, y2)
+        sl = tt(T.sl[:, :], T.ylo[:, :], T.sb[:, 15:128:16], A.add)
+        if s == 0:
+            need("v", c16, c3)
+            pcf = tt(T.pcf[:, 0:1], T.c16[:, 0:1], T.c3[:, 0:1], A.add)
+        need("v", h2, bm)
+        hx = tt(T.hxm[:, :], T.h2[:, :].indirect(T.clist[:, :]), T.bmask[:, :], A.add)
+        if s == 0:
+            for q in range(16):
+                dtw = dma("y", T.thw[q:128:16, :], T.land2[:, :, :], "dtw", a2, dow2)
+            dlw = dma("y", T.lw[0:128:16, :], T.land3[:, :, :], "dlw", a3, dow3, lwf)
+            segment(4)
+            segment(5)
+        elif s == 1:
+            segment(6)
+            segment(7)
+            letters(0)
+        else:
+            letters(1)
+            letters(2)
+    outs = letters(3)
+
+    dsy = dma("s", T.snd4[:, :, :], T.outs[0:128:16, :], "dsy", outs)
+    dow4 = dma("s", T.land4[me, :, :], T.outs[16 * me:16 * me + 1, :], "dow4")
+    need("g", dsy)
+    a4 = send(T.snd4, T.land4, "a4")
+    dla = dma("y", T.snd5[:, :, :], T.xl[:, :], "dla", xl)
+    dow5 = dma("y", T.land5[me, :, :], T.xl[16 * me:16 * me + 16, :], "dow5")
+    need("g", dla)
+    a5 = send(T.snd5, T.land5, "a5")
+    dma("s", T.syms[:, :], T.land4[:, :, :], "fsy", a4, dow4)
+    dma("y", T.last[:, :], T.land5[:, :, :], "fla", a5, dow5)
+    for sem in sorted(cnt):
+        if waited.get(sem, 0) < cnt[sem]:
+            need("g", (sem, cnt[sem]))

@@ -1,29 +1,32 @@
 from concourse.bass import DstId, RemoteDMATransfer
 from concourse.mybir import AluOpType as A, ActivationFunctionType as F
 
-I32, U16, F32, B16 = "int32", "uint16", "float32", "bfloat16"
+I32, U16, F32, B16, F16 = "int32", "uint16", "float32", "bfloat16", "float16"
 SCRATCH = {}
-for _i, _w, _t in ((0, 8, I32), (1, 16, I32), (2, 16, B16), (3, 16, B16), (4, 4, F32), (5, 1, F32)):
+for _i, _w, _t in ((0, 8, I32), (1, 16, I32), (3, 16, I32), (4, 4, F32), (5, 1, F32)):
     SCRATCH["snd%d" % _i] = SCRATCH["land%d" % _i] = ("dram", [8, 128, _w], _t)
 for _t, _l in (
-        (I32, "ic 128 ij 128 is1 128 ip 8 i2 8 i1 8 i4 4 i3o 32 cq 8 c7 8 c3 8 ch 8 c1 8 c8 8 sgi 128 i32i 32"
-              " ind4i 4 pl 32 zz 32 zh 32 loi 32 lh 32 poolw 256 wq 128 win 2048 lti 128 c0 8 k 8 lo 8 f3 8 h2 8"
-              " y 8 ylo 8 sl 8 mt 128 mf 128 mc 128 mq 128 sa 128"),
-        (U16, "permo 8 clist 8 offm 32 off 32 off0 8 off2 32"),
-        (F32, "qf 8 qs 8 p15 8 c16 8 pcf 8 maskf 128 blkf 128 bmask 128 hxm 128 sgf 128 i32f 32 ind4 4 lz 256 selx 128 g0 128"
-              " gm 128 sc 128 slm 8 u 8 u4 8 pr 8 xq 8 g256 8 xl 8 lg 512 outs 512 sp 128 mff 128 mn 128 mr 128 mv 128"),
-        (B16, "blkb 128 lt 128 e8 128 ones 128 c255 128 n255 128 idn 128 nid 128 i128 8 selw 1024 sgb 128 km 128 zer 128"
-              " lob 32 selm 512 gby 512 bw 4112 ltb 128 lw 2048 thw 2048 qb 128 maskb 128 w 8 wm 128 pp 8 ppx 432 sb 128"
-              " gb 128")):
+        (I32, "ic 128 ij 128 is1 128 il 128 ip 8 i1 8 i4 4 i3o 32 cq 8 ch 8 c1 8 c4 8 sgi 128 i32i 32"
+              " ind4i 4 pl 32 zz 32 zh 32 loi 32 lh 32 poolw 256 win 2048 c0 8 h0 8 h2 8 y 8 ylo 8 sl 8 sa 128 wq 128 tb 256"),
+        (U16, "clist 8 offm 32 off 32 off2 32"),
+        (F32, "qf 8 qs 8 p15 8 c8 8 lane 8 cf 16 maskf 128 sgf 128 zf 32 ind4 4 r1 24 r2f 32 ent0 128"
+              " pr 8 xq 8 g256 8 xl 8 spf 128"),
+        (F16, "sph 128 grh 8 r2 32 ent 512"),
+        (B16, "lt 128 idn 128 big 128 e8 128 ones 128 selw 1024 zer 8 r3 8 lob 32 selm 512 gby 512 bw 4112 w 8 wc 48 gb 128"
+              " lz 256 i32f 32")):
     _l = _l.split()
     for _i in range(0, len(_l), 2):
         SCRATCH[_l[_i]] = ("sbuf", [128, int(_l[_i + 1])], _t)
 SCRATCH["lor"] = ("sbuf", [8, 512], B16)
-for _i in ("ps0", "ps1", "ps2", "ps3", "ps4", "psr", "psz", "psb"):
+SCRATCH["outs"] = ("sbuf", [8, 512], F32)
+for _i in ("ps0", "ps1", "ps2", "ps3", "psl", "psa", "psb", "psc"):
     SCRATCH[_i] = ("psum", [128, 512], F32)
-SEMAPHORES = ["gi", "v", "t", "s", "ls", "a0", "a1", "a2", "a3", "a4", "a5",
-              "l0", "l1", "own0", "own1", "lmt", "lpl", "lzz", "llt", "dlo", "dth", "dlt", "dow2", "dow3", "dst", "dpa",
-              "dpb", "dwa", "dw", "dtw", "dlw", "dsy", "dow4", "dla", "dow5", "fsy", "fla"]
+SEMAPHORES = ["gi", "v", "t", "s", "ls", "a0", "a1", "a3", "a4", "a5",
+              "l0", "l1", "l3", "own0", "own1", "own3", "lpl", "lzz", "dlo", "dsa", "dst", "dpa",
+              "dpb", "dwa", "dwb", "dwq", "dtb", "dlw", "dsy", "dow4", "dla", "dow5", "fsy", "fla"]
+ROUND = 1.5 * 2.0 ** 34
+READS = 4352.0
+R_F, R_E, R_SLOT, R_SYM, R_ONE = 0, 1, 2, 3, 5
 
 
 def rank_program(g, core, T, topo):
@@ -66,9 +69,6 @@ def rank_program(g, core, T, topo):
     def tt(out, a, b, op):
         return V(v.tensor_tensor(out, a, b, op))
 
-    def scan(out, a, b, o1, o2):
-        return V(v.tensor_tensor_scan(out, a, b, 0.0, o1, o2))
-
     def copy(out, in_):
         return V(v.tensor_copy(out, in_))
 
@@ -77,6 +77,9 @@ def rank_program(g, core, T, topo):
 
     def act(out, in_, *sc):
         return S(ac.activation(out, in_, F.Copy, *sc))
+
+    def lin(out, in_, bias, scale):
+        return S(ac.activation(out, in_, F.Identity, bias, scale))
 
     others = [d for d in T.cores if d != core]
     near = topo.cores_of(core)
@@ -105,321 +108,279 @@ def rank_program(g, core, T, topo):
     dma("y", T.snd0[:, 16:80, :], T.stock[:, :], "l0")
     l0 = dma("s", T.snd0[:, 80:128, :], T.models[:, 0:384], "l0")
     l1 = dma("y", T.snd1[:, :, :], T.models[:, :], "l1")
-    lmt = dma("y", T.mt[:, :], T.models[:, :], "lmt")
     lpl = dma("y", T.pl[:, :], T.places[me, :], "lpl")
     for s in range(4):
         for h in range(2):
             t = 1024 * s + 512 * h
             lzz = dma("s", T.zz[32 * s:32 * s + 32, 16 * h:16 * h + 16], T.places[me, t:t + 512], "lzz")
-    llt = dma("y", T.lti[:, :], T.letters[:, :], "llt")
+    l3 = dma("y", T.snd3[:, :, :], T.letters[:, :], "l3")
     dma("y", T.land0[me, 0:16, :], T.states[me, :], "own0")
     own0 = dma("y", T.land0[me, 16:80, :], T.stock[me, :], "own0")
     own1 = dma("y", T.land1[me, :, :], T.models[me, :], "own1")
+    own3 = dma("y", T.land3[me, :, :], T.letters[me, :], "own3")
 
     def pattern(out, pat, base, mul):
         return did(g.iota(out, pat, base, mul), "gi")
 
-    def choose(out, in_, step, op, mul, *toks):
-        need("g", *toks)
-        return did(g.affine_select(out, in_, [[step, 128]], op, 0.0, 0, mul), "gi")
-
     ip = pattern(T.ip[:, 0:1], [[0, 1]], 0, 1)
     ic = pattern(T.ic[:, :], [[-16, 8], [0, 16]], 0, 1)
-    is1 = pattern(T.is1[:, :], [[1, 128]], 0, 128)
     ij = pattern(T.ij[:, :], [[0, 8], [1, 16]], 0, 0)
+    is1 = pattern(T.is1[:, :], [[1, 128]], 0, 128)
+    i4 = pattern(T.i4[:, :], [[-8, 4]], 0, 1)
     need("g", l0)
     a0 = send(T.snd0, T.land0, "a0")
     need("g", l1)
     a1 = send(T.snd1, T.land1, "a1")
-    i4 = pattern(T.i4[:, :], [[-8, 4]], 0, 1)
+    need("g", l3)
+    a3 = send(T.snd3, T.land3, "a3")
     i3o = pattern(T.i3o[:, :], [[-32, 4], [-1, 8]], 128, 1)
     i1 = pattern(T.i1[:, :], [[1, 8]], 0, 0)
-    i2 = pattern(T.i2[:, :], [[2, 8]], 0, 0)
+    il = pattern(T.il[:, :], [[1, 8], [8, 16]], 0, 0)
 
+    def row(a):
+        return T.maskf[:, a:a + 1]
+
+    def cf(i):
+        return T.cf[:, i:i + 1]
+
+    grp = T.sgf[:, 0:128:16]
     ones = fill(T.ones[:, :], 1.0)
-    fill(T.c255[:, :], 255.0)
-    n255 = fill(T.n255[:, :], -255.0)
-    lt = choose(T.lt[:, :], T.ones[:, :], 1, A.is_gt, -1, ones)
-    lz0 = fill(T.lz[:, :], 0.0)
-    need("v", ip)
+    big = fill(T.big[:, :], READS)
+    fill(T.win[:, 0:1024], 1)
+    need("g", big)
+    idn = did(g.affine_select(T.idn[:, :], T.big[:, :], [[-1, 128]], A.is_equal, 0.0, 0, 1), "gi")
+    need("v", ip, ic)
     cq = ts(T.cq[:, 0:1], T.ip[:, 0:1], 15, None, A.bitwise_and)
-    p15 = ts(T.p15[:, 0:1], T.ip[:, 0:1], 15.0, None, A.mult)
-    ch = ts(T.ch[:, 0:1], T.ip[:, 0:1], 1, 7, A.arith_shift_right, A.bitwise_and)
-    c1 = ts(T.c1[:, 0:1], T.ip[:, 0:1], 1, None, A.bitwise_and)
-    need("v", ic, p15)
     sgi = ts(T.sgi[:, :], T.ic[:, :], 4, None, A.arith_shift_right)
-    e8 = ts(T.e8[:, :], T.ic[:, :], T.p15[:, 0:1], 0.0, A.add, A.is_equal)
-    need("v", c1)
-    c8 = ts(T.c8[:, 0:1], T.c1[:, 0:1], 8.0, None, A.mult)
-    need("v", sgi)
-    sg = ts(T.sgf[:, :], T.sgi[:, :], 0.0, None, A.is_equal)
-    need("v", is1)
-    sa = ts(T.sa[:, :], T.is1[:, :], 2047, None, A.bitwise_and)
+    p15 = ts(T.p15[:, 0:1], T.ip[:, 0:1], 15.0, None, A.mult)
     need("v", cq)
     qf = copy(T.qf[:, 0:1], T.cq[:, 0:1])
-    need("v", ch, c8)
-    qs = tt(T.qs[:, 0:1], T.ch[:, 0:1], T.c8[:, 0:1], A.add)
-    need("v", sa)
-    sp = ts(T.sp[:, :], T.sa[:, :], -4095.5, None, A.add)
+    need("v", sgi)
+    sg = ts(T.sgf[:, :], T.sgi[:, :], 0.0, None, A.is_equal)
     need("v", ij, qf)
     mf = ts(T.maskf[:, :], T.ij[:, :], T.qf[:, 0:1], None, A.is_equal)
-    bf = ts(T.blkf[:, :], T.ij[:, :], 0.0, None, A.is_gt)
-    need("v", lmt)
-    mf_ = ts(T.mf[:, :], T.mt[:, :], 2.0 ** -11, 0.500244140625, A.mult, A.add)
-    mc = ts(T.mc[:, :], T.mt[:, :], 2047, None, A.bitwise_and)
+    need("v", is1, p15)
+    sa = ts(T.sa[:, :], T.is1[:, :], 2047, None, A.bitwise_and)
+    e8 = ts(T.e8[:, :], T.ic[:, :], T.p15[:, 0:1], 0.0, A.add, A.is_equal)
     need("v", lpl)
     loi = ts(T.loi[:, :], T.pl[:, :], 7, None, A.bitwise_and)
     lh = ts(T.lh[:, :], T.pl[:, :], 8, 8, A.arith_shift_right, A.bitwise_and)
-    need("v", mf_)
-    mff = copy(T.mff[:, :], T.mf[:, :])
-    need("v", mc, sp)
-    mn = tt(T.mn[:, :], T.mc[:, :], T.sp[:, :], A.subtract)
-    need("v", loi, lh)
+    fill(T.win[:, 1024:1152], 1)
+    need("v", loi, lh, mf)
     lob = tt(T.lob[:, :], T.loi[:, :], T.lh[:, :], A.add)
-    need("v", mff)
-    mr = V(v.reciprocal(T.mr[:, :], T.mff[:, :]))
-    need("v", mn, mr)
-    mv = tt(T.mv[:, :], T.mn[:, :], T.mr[:, :], A.mult)
-    need("v", lzz)
+    wf = fill(T.win[:, 1152:2048], 1)
+    need("v", lzz, i4)
     zh = ts(T.zh[:, :], T.zz[:, :], 3, 255, A.arith_shift_right, A.bitwise_and)
-    need("v", mv)
-    mq = ts(T.mq[:, :], T.mv[:, :], -256.5, None, A.add)
-    need("v", i4, i3o)
     n4i = ts(T.ind4i[:, :], T.i4[:, :], 31, 3, A.bitwise_and, A.arith_shift_right)
-    i3i = ts(T.i32i[:, :], T.i3o[:, :], 231, None, A.bitwise_and)
-    need("v", mq)
-    qb = copy(T.qb[:, :], T.mq[:, :])
-    need("v", n4i, i3i)
+    lz0 = fill(T.lz[:, :], 0.0)
+    need("v", zh, n4i)
+    copy(T.zf[:, :], T.zh[:, :])
     n4 = ts(T.ind4[:, :], T.ind4i[:, :], 0.0, None, A.is_equal)
+    ch = ts(T.ch[:, 0:1], T.ip[:, 0:1], 1, 7, A.arith_shift_right, A.bitwise_and)
+    c1 = ts(T.c1[:, 0:1], T.ip[:, 0:1], 1, None, A.bitwise_and)
+    c4 = ts(T.c4[:, 0:1], T.ip[:, 0:1], 4, None, A.arith_shift_right)
+    tt(cf(1), row(R_SLOT), row(R_E), A.subtract)
+    su = tt(cf(8), row(R_E), row(R_SLOT), A.subtract)
+    grh = copy(T.grh[:, :], grp)
+    need("v", c1)
+    c8 = ts(T.c8[:, 0:1], T.c1[:, 0:1], 8.0, None, A.mult)
+    need("v", c4, i3o)
+    c4f = copy(cf(7), T.c4[:, 0:1])
+    i3i = ts(T.i32i[:, :], T.i3o[:, :], 231, None, A.bitwise_and)
+    need("v", c8)
+    qs = tt(T.qs[:, 0:1], T.ch[:, 0:1], T.c8[:, 0:1], A.add)
+    need("v", c4f)
+    lane = ts(T.lane[:, 0:1], T.qf[:, 0:1], 8.0, cf(7), A.mult, A.add)
+    need("v", i3i)
     i3 = ts(T.i32f[:, :], T.i32i[:, :], 128.0, None, A.is_equal)
-    need("v", n4, zh, lz0)
-    lz = None
-    for b in range(8):
-        h, bb = b // 4, b % 4
-        c = 128 * h + 16 * b
-        lz = ts(T.lz[:, c:c + 16], T.zh[:, 16 * h:16 * h + 16], T.ind4[:, bb:bb + 1], None, A.mult)
+    fill(T.zer[:, :], 0.0)
+    fill(T.wc[:, 0:1], 0.0)
+    con = fill(T.bw[:, 0:1], 0.0)
     need("v", i1)
     clist = copy(T.clist[:, :], T.i1[:, :])
-    need("v", llt)
-    ltb = copy(T.ltb[:, :], T.lti[:, :])
-    i128 = fill(T.i128[:, :], 1.0 / 128)
-
-    for s in range(4):
-        dlo = dma("y", T.lor[:, 128 * s:128 * s + 128], T.lob[32 * s:32 * s + 32, :], "dlo", lob)
-    need("t", dlo, e8)
-    plo = P(te.matmul(T.ps4[:, :], T.e8[0:8, :], T.lor[:, :], True, True))
-    need("t", lz, i3)
-    te.matmul(T.psz[:, 0:32], T.lz[:, 0:128], T.i32f[:, :], True, False)
-    pz = P(te.matmul(T.psz[:, 0:32], T.lz[:, 128:256], T.i32f[:, :], False, True))
-    need("v", plo, qs)
-    selm = ts(T.selm[:, :], T.ps4[:, :], T.qs[:, 0:1], None, A.is_equal)
-
-    dth = dma("y", T.snd2[:, :, :], T.qb[:, :], "dth", qb)
-    dow2 = dma("y", T.land2[me, :, :], T.qb[16 * me:16 * me + 16, :], "dow2")
-    need("g", dth)
-    a2 = send(T.snd2, T.land2, "a2")
-    choose(T.idn[:, :], T.c255[:, :], -1, A.is_equal, 1, n255)
-    nid = choose(T.nid[:, :], T.n255[:, :], -1, A.is_equal, 1)
+    need("v", il, lane)
+    lt = ts(T.lt[:, :], T.il[:, :], T.lane[:, 0:1], None, A.is_gt)
 
     need("s", ones, sg)
     for b in range(8):
-        act(T.selw[:, 128 * b:128 * b + 128], T.ones[:, :], 0.0, T.sgf[:, 16 * b:16 * b + 1])
-    se = act(T.sgb[:, :], T.sgf[:, :])
-    need("s", se)
-    act(T.lw[:, 0:1024], T.selw[:, :])
+        se = act(T.selw[:, 128 * b:128 * b + 128], T.ones[:, :], 0.0, T.sgf[:, 16 * b:16 * b + 1])
+    need("s", mf)
+    t = act(cf(0), row(R_F), 0.0, 2.0 ** -11)
+    act(cf(5), row(R_F), 0.0, -1023.5)
+    rnd = act(cf(6), row(R_F), 0.0, ROUND)
+    r3 = act(T.r3[:, :], grp, 0.0, 1.0 / 16)
+    need("s", n4, lz0)
+    for b in range(8):
+        h, bb = b // 4, b % 4
+        c = 128 * h + 16 * b
+        lz = act(T.lz[:, c:c + 16], T.zf[:, 16 * h:16 * h + 16], 0.0, T.ind4[:, bb:bb + 1])
+    need("s", t, su)
+    lin(cf(2), row(R_ONE), cf(0), 1.0 - ROUND / 2048)
+    lin(cf(3), row(R_ONE), cf(1), -2048.0)
+    lin(cf(4), row(R_ONE), cf(8), 6144.0)
+    lin(cf(9), row(R_ONE), row(R_F), 1.0)
+    t = lin(cf(10), row(R_ONE), cf(8), 4096.0)
+
+    for s in range(4):
+        dlo = dma("y", T.lor[:, 128 * s:128 * s + 128], T.lob[32 * s:32 * s + 32, :], "dlo", lob)
+    dsa = dma("y", T.win[R_SLOT:128:16, :], T.sa[:, :], "dsa", wf, sa)
+    need("t", dlo, e8)
+    plo = P(te.matmul(T.psl[:, :], T.e8[0:8, :], T.lor[:, :], True, True))
+    need("t", lz, i3)
+    te.matmul(T.psb[:, 0:32], T.lz[:, 0:128], T.i32f[:, :], True, False)
+    pz = P(te.matmul(T.psb[:, 0:32], T.lz[:, 128:256], T.i32f[:, :], False, True))
+    need("v", plo, qs)
+    selm = ts(T.selm[:, :], T.psl[:, :], T.qs[:, 0:1], None, A.is_equal)
+    need("v", pz)
+    offm = copy(T.offm[:, :], T.psb[:, 0:32])
 
     need("s", a0, own0)
     dst = dma("y", T.c0[:, :], T.land0[:, 0:16, :], "dst", a0, own0)
     for b in range(4):
         dpb = dma("s", T.poolw[16 * b:16 * b + 16, :], T.land0[:, 16:80, :], "dpb")
         dpa = dma("y", T.poolw[16 * b + 64:16 * b + 80, :], T.land0[:, 16:80, :], "dpa")
-    dwa = dma("y", T.wq[:, :], T.land1[:, :, :], "dwa", a1, own1)
-    for q in range(16):
-        dw = dma("y", T.win[q:128:16, :], T.land1[:, :, :], "dw")
-    need("s", mf, bf)
-    mb = act(T.maskb[:, :], T.maskf[:, :])
-    bb = act(T.blkb[:, :], T.blkf[:, :])
-    dlt = dma("s", T.snd3[:, :, :], T.ltb[:, :], "dlt", ltb)
-    dow3 = dma("s", T.land3[me, :, :], T.ltb[16 * me:16 * me + 16, :], "dow3")
-    need("g", dlt)
-    a3 = send(T.snd3, T.land3, "a3")
-    lwf = act(T.lw[:, 1024:2048], T.selw[:, :])
+    dwa = dma("y", T.win[R_F:128:16, :], T.land1[:, :, :], "dwa", a1, own1)
+    dwb = dma("s", T.win[R_E:128:16, :], T.land1[:, :, :], "dwb", a1, own1, wf)
+    dwq = dma("y", T.wq[:, :], T.land1[:, :, :], "dwq")
+    need("s", t)
+    for i in range(3):
+        r1 = act(T.r1[:, 8 * i:8 * i + 8], grp, 0.0, cf(2 + i))
+    for i, x in enumerate((cf(9), cf(1), cf(10), row(R_SYM))):
+        r2f = act(T.r2f[:, 8 * i:8 * i + 8], grp, 0.0, x)
+    need("v", r2f)
+    r2 = copy(T.r2[:, :], T.r2f[:, :])
+
+    gby, kept, bank = {}, {}, [None] * 4
+
+    def gather(s):
+        gby[s] = tt(T.gby[:, 128 * s:128 * s + 128], T.poolw[:, :].indirect(T.offm[:, 8 * s:8 * s + 8]),
+                    T.selm[:, 128 * s:128 * s + 128], A.mult)
+
+    def segment(s, b0, n, i):
+        need("t", gby[s], se, *([bank[i]] if bank[i] else []))
+        for k in range(n):
+            p = P(te.matmul(T["ps%d" % i][:, 128 * k:128 * k + 128], T.selw[:, 128 * (b0 + k):128 * (b0 + k + 1)],
+                            T.gby[:, 128 * s:128 * s + 128], True, True))
+        return s, b0, n, i, p
+
+    def keep(s, b0, n, i, p):
+        need("s", p)
+        t = 1 + 1024 * s + 128 * b0
+        kept[s] = bank[i] = act(T.bw[:, t:t + 128 * n], T["ps%d" % i][:, 0:128 * n])
+
+    def look(s):
+        return copy(T.ent[:, 128 * s:128 * s + 128], T.win[:, :].indirect(T.off[:, 8 * s:8 * s + 8]))
+
+    def letters(s, *toks):
+        need("t", *toks)
+        for c in range(8):
+            p = P(te.matmul(T.psl[0:8, 128 * s + c:128 * s + 128:8], T.r2[:, 24:32],
+                            T.ent[:, 128 * s + 16 * c:128 * s + 16 * c + 16], True, True))
+        return p
+
+    def symbols(s0, s1, p):
+        need("s", p)
+        return act(T.outs[:, 128 * s0:128 * s1], T.psl[0:8, 128 * s0:128 * s1])
+
+    def spread(out, tile):
+        return tt(out[:, :], tile[:, :].indirect(T.clist[:, :]), T.maskf[:, :], A.mult)
 
     need("v", dst)
-    kt = ts(T.k[:, :], T.c0[:, :], 7, 15, A.arith_shift_right, A.bitwise_and)
-    lo = ts(T.lo[:, :], T.c0[:, :], 127, None, A.bitwise_and)
     sl = ts(T.sl[:, :], T.c0[:, :], 2047, None, A.bitwise_and)
-    need("v", kt, mf, clist)
-    km = tt(T.km[:, :], T.k[:, :].indirect(T.clist[:, :]), T.maskf[:, :], A.mult)
-    need("t", km, se)
-    pk = P(te.matmul(T.psb[:, 0:128], T.sgb[:, :], T.km[:, :], True, True))
-    need("v", lo)
-    off0 = copy(T.off0[:, :], T.lo[:, :])
-    h2 = ts(T.h2[:, :], T.c0[:, :], 2.0 ** -11, 2047.500244140625, A.mult, A.add)
-    need("v", pz)
-    offm = copy(T.offm[:, :], T.psz[:, 0:32])
+    h0 = ts(T.h0[:, :], T.c0[:, :], 2.0 ** -11, -0.499755859375, A.mult, A.add)
+    need("v", sl)
+    off = copy(T.off[:, 0:8], T.sl[:, :])
+    need("v", h0, clist)
+    t = spread(T.sph, T.h0)
+    need("t", t, grh)
+    ph = P(te.matmul(T.psc[:, 0:8], T.sph[:, :], T.grh[:, :], True, True))
+    need("v", dpa, dpb, offm, selm)
+    gather(0)
+    keep(*segment(0, 0, 2, 0))
+    keep(*segment(0, 2, 2, 1))
+    need("v", ph)
+    h2 = ts(T.h2[:, :], T.psc[:, 0:8], 2048.0, None, A.add)
 
-    gby, segc, offs, ends = {}, {}, {}, {}
-
-    def gather(s0, s1):
-        r = tt(T.gby[:, 128 * s0:128 * s1], T.poolw[:, :].indirect(T.offm[:, 8 * s0:8 * s1]),
-               T.selm[:, 128 * s0:128 * s1], A.mult)
-        for s in range(s0, s1):
-            gby[s] = r
-
-    def segment(i):
-        ps = T["ps%d" % (i % 5)]
-        s, p = i // 2, None
-        need("t", gby[s], se)
-        if i >= 5:
-            need("t", segc[i - 5])
-        for k in range(4):
-            b = 4 * (i % 2) + k
-            p = P(te.matmul(ps[:, 128 * k:128 * k + 128], T.selw[:, 128 * b:128 * b + 128],
-                            T.gby[:, 128 * s:128 * s + 128], True, True))
-        need("s", p)
-        segc[i] = act(T.bw[:, 1 + 512 * i:513 + 512 * i], ps[:, :])
-
-    def letters(s):
-        need("s", offs[s], dlw, permo)
-        lg = T.lg[:, 128 * s:128 * s + 128]
-        need("s", act(lg, T.lw[:, :].indirect(T.off[:, 8 * s:8 * s + 8])))
-        return act(T.outs[:, 128 * s:128 * s + 128], lg.indirect(T.permo[:, :]))
-
-    prev, py = None, None
     for s in range(4):
-        c, x = 8 * s, 144 * (s - 1)
-        E = T.sc[:, 15:128:16]
-        need("v", sl)
-        offs[s] = copy(T.off[:, c:c + 8], T.sl[:, :])
-        slm = ts(T.slm[:, :], T.sl[:, :], -2048.0, None, A.add)
-        if s > 0:
-            need("t", prev, ones)
-            for j in range(s):
-                te.matmul(T.psb[:, 0:1], T.ones[:, :], ends[j], j == 0, False)
+        c = 8 * s
         if s == 0:
-            need("v", pk)
-            selx = ts(T.selx[:, :], T.psb[:, 0:128], T.qf[:, 0:1], None, A.is_equal)
-            need("v", off0, selx, dwa)
-            t = tt(T.g0[:, :], T.wq[:, :].indirect(T.off0[:, :]), T.selx[:, :], A.mult)
-            need("t", t, sg)
-            t = P(te.matmul(T.psr[:, 0:128], T.sgf[:, :], T.g0[:, :], True, True))
-            need("v", dpa, dpb, offm, selm)
-            gather(0, 1)
-            segment(0)
-            segment(1)
-            gather(1, 3)
-            need("v", t, mf)
-            py = gm = tt(T.gm[:, :], T.psr[:, 0:128], T.maskf[:, :], A.mult)
-            zer = fill(T.zer[:, :], 0.0)
-            need("v", gm, bf)
-            e = scan(T.sc[:, :], T.blkf[:, :], T.gm[:, :], A.mult, A.add)
-            bm = ts(T.bmask[:, :], T.maskf[:, :], -6400.0, 4096.0, A.mult, A.add)
-            zp = fill(T.ppx[:, 15:432:144], 0.0)
-            need("v", e)
-            f3 = ts(T.f3[:, :], E, 2.0 ** -11, 0.500244140625, A.mult, A.add)
-            need("v", slm)
-            u = tt(T.u[:, :], T.slm[:, :], E, A.subtract)
-            c7 = ts(T.c7[:, 0:1], T.ip[:, 0:1], 7, None, A.bitwise_and)
-            need("v", f3, h2)
-            pr = tt(T.pr[:, :], T.f3[:, :], T.h2[:, :], A.mult)
-            need("v", u)
-            u4 = ts(T.u4[:, :], T.u[:, :], -1.0, 4096.0, A.mult, A.add)
-            con = fill(T.bw[:, 0:1], 0.0)
-            need("v", pr, u4)
-            w = tt(T.w[:, :], T.pr[:, :], T.u4[:, :], A.is_lt)
-            xq = tt(T.xq[:, :], T.pr[:, :], T.u[:, :], A.add)
-            need("v", w, zer)
-            ppc, ends[s] = T.pp[:, :], T.pp[:, 7:8]
-            pp = scan(ppc, T.w[:, :], T.zer[:, 0:8], A.add, A.max)
-            g256 = ts(T.g256[:, :], T.w[:, :], 255.0, 1.0, A.mult, A.add)
-            need("v", clist, mb)
-            wm = tt(T.wm[:, :], T.w[:, :].indirect(T.clist[:, :]), T.maskb[:, :], A.mult)
+            need("v", off, rnd, dwa, dwb, dsa)
+            ent = ts(T.ent0[:, :], T.win[:, :].indirect(T.off[:, 0:8]), cf(5), cf(6), A.add, A.add)
+            need("t", ent, r1)
+            pe = P(te.matmul(T.psa[:, 0:24], T.ent0[:, :], T.r1[:, :], True, True))
+            dlw = dma("y", T.win[R_SYM:128:16, :], T.land3[:, :, :], "dlw", a3, own3, ent)
+            keep(*segment(0, 4, 2, 2))
+            keep(*segment(0, 6, 2, 3))
+            need("v", dwq)
+            ts(T.tb[:, 0:128], T.wq[:, :], 11, None, A.arith_shift_right)
+            t = ts(T.tb[:, 128:256], T.wq[:, :], 2047, None, A.bitwise_and)
+            dma("y", T.win[R_F:128:16, :], T.tb[:, 0:128], "dtb", t)
+            dtb = dma("y", T.win[R_E:128:16, :], T.tb[:, 128:256], "dtb")
+            gather(1)
         else:
-            need("v", offs[s], hx, dw)
-            gm = tt(T.gm[:, :], T.win[:, :].indirect(T.off[:, c:c + 8]), T.maskf[:, :], A.mult)
-            need("v", dtw)
-            wm = tt(T.wm[:, :], T.thw[:, :].indirect(T.off[:, c:c + 8]), T.hxm[:, :], A.is_ge)
-            need("v", gm)
-            e = scan(T.sc[:, :], T.blkf[:, :], T.gm[:, :], A.mult, A.add)
-            need("v", wm)
-            pp = scan(T.ppx[:, x + 16:x + 144], T.wm[:, :], T.zer[:, :], A.add, A.max)
-            ppc, ends[s] = T.ppx[:, x + 31:x + 144:16], T.ppx[:, x + 143:x + 144]
-            need("v", e)
-            f3 = ts(T.f3[:, :], E, 2.0 ** -11, 0.500244140625, A.mult, A.add)
-            need("v", slm)
-            u = tt(T.u[:, :], T.slm[:, :], E, A.subtract)
-            need("v", f3, h2)
-            pr = tt(T.pr[:, :], T.f3[:, :], T.h2[:, :], A.mult)
-        need("t", pp, lt)
-        base = P(te.matmul(T.psb[:, 0:1], T.lt[:, :], ends[s], s == 0, True))
-        if s == 0:
-            segment(2)
-            segment(3)
-            need("v", xq, g256)
-            y = tt(T.y[:, :], T.xq[:, :], T.g256[:, :], A.mult)
-        else:
-            need("t", i128, nid, zp, py)
-            te.matmul(T.psr[:, 0:8], T.idn[:, :], ppc, True, False)
-            te.matmul(T.psr[:, 0:8], T.nid[:, :], T.ppx[:, x + 15:x + 128:16], False, False)
-            pg = P(te.matmul(T.psr[:, 0:8], T.ones[:, :], T.i128[:, :], False, True))
-        need("v", base, con)
-        prev = ts(T.off2[:, c:c + 8], ppc, T.psb[:, 0:1], None, A.add)
-        if s > 0:
-            need("v", pr, u)
-            xq = tt(T.xq[:, :], T.pr[:, :], T.u[:, :], A.add)
+            need("v", off, dlw, dtb)
+            ent = look(s)
+            need("t", ent, r2)
+            pe = P(te.matmul(T.psa[:, 0:24], T.ent[:, 128 * s:128 * s + 128], T.r2[:, 0:24], True, True))
+            if s == 1:
+                gather(3)
+                letters(1, selm)
+            elif s == 2:
+                sym = symbols(0, 3, letters(2))
+            else:
+                sym = symbols(3, 4, letters(3, sym))
+        need("v", pe, h2)
+        pr = tt(T.pr[:, :], T.psa[:, 0:8], T.h2[:, :], A.mult)
+        need("v", pr)
+        w = tt(T.w[:, :], T.pr[:, :], T.psa[:, 16:24], A.is_lt)
+        xq = tt(T.xq[:, :], T.pr[:, :], T.psa[:, 8:16], A.add)
+        need("v", w, con)
+        wc = V(v.tensor_tensor_scan(T.wc[:, c + 1:c + 9], T.w[:, :], T.zer[:, :], T.wc[:, c:c + 1], A.add, A.add))
+        g256 = ts(T.g256[:, :], T.w[:, :], 255.0, 1.0, A.mult, A.add)
+        need("t", w, lt, idn)
+        te.matmul(T.psb[:, 0:8], T.lt[:, :], T.w[:, :], True, False)
+        te.matmul(T.psb[:, 0:8], T.idn[:, :], T.w[:, :], False, False)
+        need("t", wc)
+        cn = P(te.matmul(T.psb[:, 0:8], T.ones[:, :], T.wc[:, c:c + 8], False, True))
+        need("v", g256)
+        y = tt(T.y[:, :], T.xq[:, :], T.g256[:, :], A.mult)
+        if s < 3:
+            need("v", y)
+            ylo = ts(T.ylo[:, :], T.y[:, :], 2047, None, A.bitwise_and)
+        need("v", cn)
+        off2 = ts(T.off2[:, c:c + 8], T.psb[:, 0:8], 1.0 - READS, None, A.add)
+        need("s", off2, con, kept[s])
+        gb = act(T.gb[:, :], T.bw[:, 0:1025 + 1024 * s].indirect(T.off2[:, c:c + 8]))
+        if s < 3:
+            need("v", ylo)
+            t = spread(T.sph, T.ylo)
+            h2 = ts(T.h2[:, :], T.y[:, :], 2.0 ** -11, -0.499755859375, A.mult, A.add)
+            p0 = segment(s + 1, 0, 4, 2 * (s % 2))
+            need("t", t)
+            te.matmul(T.psc[:, 0:8], T.sph[:, :], T.grh[:, :], True, False)
         else:
             need("v", y)
-            h2 = ts(T.h2[:, :], T.y[:, :], 2.0 ** -11, 2047.500244140625, A.mult, A.add)
-            y2 = ts(T.ylo[:, :], T.y[:, :], 2047, None, A.bitwise_and)
-        need("v", prev, wm, segc[2 * s + 1])
-        t = tt(T.gb[:, :], T.bw[:, 0:1025 + 1024 * s].indirect(T.off2[:, c:c + 8]), T.wm[:, :], A.mult)
-        if s > 0:
-            need("v", xq, pg)
-            py = y = tt(T.y[:, :], T.xq[:, :], T.psr[:, 0:8], A.mult)
-        if s == 1:
-            need("v", i2, pcf)
-            permo = ts(T.permo[:, :], T.i2[:, :], T.pcf[:, 0:1], None, A.add)
+            t = spread(T.spf, T.y)
+            need("t", t)
+            te.matmul(T.psc[:, 0:8], T.spf[:, :], grp, True, False)
+        need("t", gb, r3)
+        pb = P(te.matmul(T.psc[:, 0:8], T.gb[:, :], T.r3[:, :], False, True))
         if s == 0:
-            gather(3, 4)
-            c3 = ts(T.c3[:, 0:1], T.ip[:, 0:1], 3, 1, A.arith_shift_right, A.bitwise_and)
-        need("v", t, bb)
-        t = scan(T.sb[:, :], T.blkb[:, :], T.gb[:, :], A.mult, A.add)
-        if s == 3:
-            need("v", t, y)
-            xl = tt(T.xl[:, :], T.y[:, :], T.sb[:, 15:128:16], A.add)
-            break
-        if s > 0:
-            need("v", y)
-            y2 = ts(T.ylo[:, :], T.y[:, :], 2047, None, A.bitwise_and)
-            h2 = ts(T.h2[:, :], T.y[:, :], 2.0 ** -11, 2047.500244140625, A.mult, A.add)
-        else:
-            need("v", c7)
-            c16 = ts(T.c16[:, 0:1], T.c7[:, 0:1], 16.0, None, A.mult)
-        need("v", t, y2)
-        sl = tt(T.sl[:, :], T.ylo[:, :], T.sb[:, 15:128:16], A.add)
-        if s == 0:
-            need("v", c16, c3)
-            pcf = tt(T.pcf[:, 0:1], T.c16[:, 0:1], T.c3[:, 0:1], A.add)
-        need("v", h2, bm)
-        hx = tt(T.hxm[:, :], T.h2[:, :].indirect(T.clist[:, :]), T.bmask[:, :], A.add)
-        if s == 0:
-            for q in range(16):
-                dtw = dma("y", T.thw[q:128:16, :], T.land2[:, :, :], "dtw", a2, dow2)
-            dlw = dma("y", T.lw[0:128:16, :], T.land3[:, :, :], "dlw", a3, dow3, lwf)
-            segment(4)
-            segment(5)
+            gather(2)
         elif s == 1:
-            segment(6)
-            segment(7)
-            letters(0)
-        else:
-            letters(1)
-            letters(2)
-    outs = letters(3)
+            late = look(0)
+        need("v", pb)
+        if s == 3:
+            xl = copy(T.xl[:, :], T.psc[:, 0:8])
+            break
+        off = copy(T.off[:, c + 8:c + 16], T.psc[:, 0:8])
+        keep(*p0)
+        keep(*segment(s + 1, 4, 4, 2 * (s % 2) + 1))
+        if s == 1:
+            letters(0, late)
 
-    dsy = dma("s", T.snd4[:, :, :], T.outs[0:128:16, :], "dsy", outs)
-    dow4 = dma("s", T.land4[me, :, :], T.outs[16 * me:16 * me + 1, :], "dow4")
+    dsy = dma("y", T.snd4[:, :, :], T.outs[:, :], "dsy", sym)
+    dow4 = dma("y", T.land4[me, :, :], T.outs[me:me + 1, :], "dow4")
     need("g", dsy)
     a4 = send(T.snd4, T.land4, "a4")
     dla = dma("y", T.snd5[:, :, :], T.xl[:, :], "dla", xl)

@@ -6,27 +6,27 @@ SCRATCH = {}
 for _i, _w, _t in ((0, 8, I32), (1, 16, I32), (3, 16, I32), (4, 4, F32), (5, 1, F32)):
     SCRATCH["snd%d" % _i] = SCRATCH["land%d" % _i] = ("dram", [8, 128, _w], _t)
 for _t, _l in (
-        (I32, "ic 128 ij 128 is1 128 il 128 ip 8 i1 8 i4 4 i3o 32 cq 8 ch 8 c1 8 c4 8 sgi 128 i32i 32"
-              " ind4i 4 pl 32 zz 32 zh 32 loi 32 lh 32 poolw 256 win 2048 c0 8 h0 8 h2 8 y 8 ylo 8 sl 8 sa 128 wq 128 tb 256"),
-        (U16, "clist 8 offm 32 off 32 off2 32"),
-        (F32, "qf 8 qs 8 p15 8 c8 8 lane 8 cf 16 maskf 128 sgf 128 zf 32 ind4 4 r1 24 r2f 32 ent0 128"
-              " pr 8 xq 8 g256 8 xl 8 spf 128"),
-        (F16, "sph 128 grh 8 r2 32 ent 512"),
-        (B16, "lt 128 idn 128 big 128 e8 128 ones 128 selw 1024 zer 8 r3 8 lob 32 selm 512 gby 512 bw 4112 w 8 wc 48 gb 128"
-              " lz 256 i32f 32")):
+        (I32, "ij 128 is1 128 il 128 ip 8 pi 8"
+              " pl 32 zz 32 zh 32 loi 32 poolw 256 win 2048 c0 8 h0 8 h2 8 y 8 ylo 8 sl 8 wq 128 tb 256"),
+        (U16, "clist 8 permo 8 offm 32 off 32 off2 32"),
+        (F32, "pf 8 cf 24 maskf 128 grp 8 zf 32 lh 32 ind4 4 r1 24 r2 16 ent 512 onef 128 con 24 pr 8 xq 8 z 8 xl 8"
+              " spf 128 hr 128 outs 512"),
+        (F16, "sph 128 grh 8 hx 128"),
+        (B16, "lt 128 idn 128 big 128 e8 128 ones 128 selw 256 zer 8 r3 8 lob 32 selm 512 gby 512 bw 4112 w 16 wc 48 gb 128"
+              " lz 256 i32f 32 tot 8")):
     _l = _l.split()
     for _i in range(0, len(_l), 2):
         SCRATCH[_l[_i]] = ("sbuf", [128, int(_l[_i + 1])], _t)
 SCRATCH["lor"] = ("sbuf", [8, 512], B16)
-SCRATCH["outs"] = ("sbuf", [8, 512], F32)
 for _i in ("ps0", "ps1", "ps2", "ps3", "psl", "psa", "psb", "psc"):
     SCRATCH[_i] = ("psum", [128, 512], F32)
-SEMAPHORES = ["gi", "v", "t", "s", "ls", "a0", "a1", "a3", "a4", "a5",
-              "l0", "l1", "l3", "own0", "own1", "own3", "lpl", "lzz", "dlo", "dsa", "dst", "dpa",
-              "dpb", "dwa", "dwb", "dwq", "dtb", "dlw", "dsy", "dow4", "dla", "dow5", "fsy", "fla"]
+SEMAPHORES = ["gi", "v", "t", "s", "ls", "a0", "a1", "a3", "a4", "a5", "l3", "dtb", "dlw",
+              "l0", "l1", "own0", "own1", "own3", "lpl", "lzz", "dlo", "dst", "dpa",
+              "dpb", "dwa", "dwb", "dwq", "dsy", "dow4", "dla", "dow5", "fsy", "fla"]
 ROUND = 1.5 * 2.0 ** 34
-READS = 4352.0
-R_F, R_E, R_SLOT, R_SYM, R_ONE = 0, 1, 2, 3, 5
+READS = 8192.0
+SHIFTS = False
+R_F, R_E, R_SLOT, R_SYM = 0, 1, 2, 3
 
 
 def rank_program(g, core, T, topo):
@@ -122,20 +122,20 @@ def rank_program(g, core, T, topo):
     def pattern(out, pat, base, mul):
         return did(g.iota(out, pat, base, mul), "gi")
 
+    is1 = pattern(T.is1[:, :], [[1, 128]], 0, 0)
     ip = pattern(T.ip[:, 0:1], [[0, 1]], 0, 1)
-    ic = pattern(T.ic[:, :], [[-16, 8], [0, 16]], 0, 1)
-    ij = pattern(T.ij[:, :], [[0, 8], [1, 16]], 0, 0)
-    is1 = pattern(T.is1[:, :], [[1, 128]], 0, 128)
-    i4 = pattern(T.i4[:, :], [[-8, 4]], 0, 1)
+    ones = fill(T.ones[:, :], 1.0)
+    big = fill(T.big[:, :], READS)
+    need("g", big)
+    e8 = did(g.affine_select(T.e8[:, :], T.ones[:, :], [[-1, 8], [0, 16]], A.is_equal, 0.0, 0, 1), "gi")
     need("g", l0)
     a0 = send(T.snd0, T.land0, "a0")
     need("g", l1)
     a1 = send(T.snd1, T.land1, "a1")
     need("g", l3)
     a3 = send(T.snd3, T.land3, "a3")
-    i3o = pattern(T.i3o[:, :], [[-32, 4], [-1, 8]], 128, 1)
-    i1 = pattern(T.i1[:, :], [[1, 8]], 0, 0)
     il = pattern(T.il[:, :], [[1, 8], [8, 16]], 0, 0)
+    idn = did(g.affine_select(T.idn[:, :], T.big[:, :], [[-1, 128]], A.is_equal, 0.0, 0, 1), "gi")
 
     def row(a):
         return T.maskf[:, a:a + 1]
@@ -143,112 +143,112 @@ def rank_program(g, core, T, topo):
     def cf(i):
         return T.cf[:, i:i + 1]
 
-    grp = T.sgf[:, 0:128:16]
-    ones = fill(T.ones[:, :], 1.0)
-    big = fill(T.big[:, :], READS)
-    fill(T.win[:, 0:1024], 1)
-    need("g", big)
-    idn = did(g.affine_select(T.idn[:, :], T.big[:, :], [[-1, 128]], A.is_equal, 0.0, 0, 1), "gi")
-    need("v", ip, ic)
-    cq = ts(T.cq[:, 0:1], T.ip[:, 0:1], 15, None, A.bitwise_and)
-    sgi = ts(T.sgi[:, :], T.ic[:, :], 4, None, A.arith_shift_right)
-    p15 = ts(T.p15[:, 0:1], T.ip[:, 0:1], 15.0, None, A.mult)
-    need("v", cq)
-    qf = copy(T.qf[:, 0:1], T.cq[:, 0:1])
-    need("v", sgi)
-    sg = ts(T.sgf[:, :], T.sgi[:, :], 0.0, None, A.is_equal)
-    need("v", ij, qf)
-    mf = ts(T.maskf[:, :], T.ij[:, :], T.qf[:, 0:1], None, A.is_equal)
-    need("v", is1, p15)
-    sa = ts(T.sa[:, :], T.is1[:, :], 2047, None, A.bitwise_and)
-    e8 = ts(T.e8[:, :], T.ic[:, :], T.p15[:, 0:1], 0.0, A.add, A.is_equal)
-    need("v", lpl)
-    loi = ts(T.loi[:, :], T.pl[:, :], 7, None, A.bitwise_and)
-    lh = ts(T.lh[:, :], T.pl[:, :], 8, 8, A.arith_shift_right, A.bitwise_and)
-    fill(T.win[:, 1024:1152], 1)
-    need("v", loi, lh, mf)
-    lob = tt(T.lob[:, :], T.loi[:, :], T.lh[:, :], A.add)
-    wf = fill(T.win[:, 1152:2048], 1)
-    need("v", lzz, i4)
-    zh = ts(T.zh[:, :], T.zz[:, :], 3, 255, A.arith_shift_right, A.bitwise_and)
-    n4i = ts(T.ind4i[:, :], T.i4[:, :], 31, 3, A.bitwise_and, A.arith_shift_right)
-    lz0 = fill(T.lz[:, :], 0.0)
-    need("v", zh, n4i)
-    copy(T.zf[:, :], T.zh[:, :])
-    n4 = ts(T.ind4[:, :], T.ind4i[:, :], 0.0, None, A.is_equal)
-    ch = ts(T.ch[:, 0:1], T.ip[:, 0:1], 1, 7, A.arith_shift_right, A.bitwise_and)
-    c1 = ts(T.c1[:, 0:1], T.ip[:, 0:1], 1, None, A.bitwise_and)
-    c4 = ts(T.c4[:, 0:1], T.ip[:, 0:1], 4, None, A.arith_shift_right)
-    tt(cf(1), row(R_SLOT), row(R_E), A.subtract)
-    su = tt(cf(8), row(R_E), row(R_SLOT), A.subtract)
-    grh = copy(T.grh[:, :], grp)
-    need("v", c1)
-    c8 = ts(T.c8[:, 0:1], T.c1[:, 0:1], 8.0, None, A.mult)
-    need("v", c4, i3o)
-    c4f = copy(cf(7), T.c4[:, 0:1])
-    i3i = ts(T.i32i[:, :], T.i3o[:, :], 231, None, A.bitwise_and)
-    need("v", c8)
-    qs = tt(T.qs[:, 0:1], T.ch[:, 0:1], T.c8[:, 0:1], A.add)
-    need("v", c4f)
-    lane = ts(T.lane[:, 0:1], T.qf[:, 0:1], 8.0, cf(7), A.mult, A.add)
-    need("v", i3i)
-    i3 = ts(T.i32f[:, :], T.i32i[:, :], 128.0, None, A.is_equal)
+    grp = T.grp[:, :]
+
+    def slots(k0, k1):
+        for k in range(k0, k1):
+            t = ts(T.win[:, 128 * k:128 * k + 128], T.is1[:, :], 128.0 * k, None, A.add)
+        return t
+
+    fill(T.lz[:, :], 0.0)
     fill(T.zer[:, :], 0.0)
     fill(T.wc[:, 0:1], 0.0)
     con = fill(T.bw[:, 0:1], 0.0)
-    need("v", i1)
-    clist = copy(T.clist[:, :], T.i1[:, :])
-    need("v", il, lane)
-    lt = ts(T.lt[:, :], T.il[:, :], T.lane[:, 0:1], None, A.is_gt)
+    hx = fill(T.hx[:, :], 1.0)
+    need("s", ones)
+    act(T.onef[0:1, :], T.ones[0:1, :])
+    for i, x in enumerate((6144.0, 1.0 - ROUND / 2048, -2048.0)):
+        cst = act(T.con[0:1, 8 * i:8 * i + 8], T.ones[0:1, 0:8], 0.0, x)
+    need("v", is1)
+    ts(T.ij[:, :], T.is1[:, :], 15, None, A.bitwise_and)
+    need("v", ip)
+    for i, (sh, m) in enumerate(((0, 15), (4, 7), (4, 1), (3, 3), (5, 3), (0, 7))):
+        t = ts(T.pi[:, i:i + 1], T.ip[:, 0:1], sh, m, A.arith_shift_right, A.bitwise_and)
+    slots(0, 1)
+    need("v", t)
+    pf = copy(T.pf[:, 0:6], T.pi[:, 0:6])
+    qf = T.pf[:, 0:1]
+    need("s", pf)
+    act(T.selw[:, 128:256], T.ones[:, :], 0.0, T.pf[:, 2:3])
+    i3c = lin(cf(7), T.pf[:, 4:5], T.pf[:, 5:6], 8.0)
+    qh = act(cf(12), qf, 0.0, 0.5)
+    lane = lin(cf(13), qf, T.pf[:, 1:2], 8.0)
+    slots(1, 2)
+    need("v", pf)
+    ts(grp, T.is1[:, 0:8], T.pf[:, 1:2], None, A.is_equal)
+    ts(T.ind4[:, :], T.is1[:, 0:4], T.pf[:, 3:4], None, A.is_equal)
+    ts(cf(17), qf, 8.0, -127.0, A.is_ge, A.mult)
+    mf = ts(T.maskf[:, :], T.ij[:, :], qf, None, A.is_equal)
+    slots(2, 4)
+    need("v", lpl)
+    loi = ts(T.loi[:, :], T.pl[:, :], 7, None, A.bitwise_and)
+    lh = ts(T.lh[:, :], T.pl[:, :], 2048.0, 0.5, A.is_ge, A.mult)
+    slots(4, 5)
+    need("v", lh)
+    lob = tt(T.lob[:, :], T.loi[:, :], T.lh[:, :], A.add)
+    slots(5, 8)
+    need("v", lzz)
+    zh = ts(T.zh[:, :], T.zz[:, :], 3, 255, A.arith_shift_right, A.bitwise_and)
+    slots(8, 9)
+    need("v", zh, i3c)
+    zf = copy(T.zf[:, :], T.zh[:, :])
+    i3 = ts(T.i32f[:, :], T.is1[:, 0:32], cf(7), None, A.is_equal)
+    wf = slots(9, 16)
+    grh = copy(T.grh[:, :], grp)
+    clist = copy(T.clist[:, :], T.is1[:, 0:8])
 
-    need("s", ones, sg)
-    for b in range(8):
-        se = act(T.selw[:, 128 * b:128 * b + 128], T.ones[:, :], 0.0, T.sgf[:, 16 * b:16 * b + 1])
     need("s", mf)
-    t = act(cf(0), row(R_F), 0.0, 2.0 ** -11)
+    act(cf(0), row(R_F), 0.0, 2.0 ** -11)
+    act(cf(14), row(R_E), 0.0, -1.0)
+    t = act(cf(15), row(R_SLOT), 0.0, -1.0)
     act(cf(5), row(R_F), 0.0, -1023.5)
+    act(cf(16), row(R_F), 0.0, -1024.0)
     rnd = act(cf(6), row(R_F), 0.0, ROUND)
+    need("s", t)
+    se = lin(T.selw[:, 0:128], T.selw[:, 128:256], 1.0, -1.0)
+    lin(cf(1), row(R_SLOT), cf(14), 1.0)
+    t = lin(cf(8), row(R_E), cf(15), 1.0)
     r3 = act(T.r3[:, :], grp, 0.0, 1.0 / 16)
-    need("s", n4, lz0)
+    need("s", zf)
     for b in range(8):
         h, bb = b // 4, b % 4
         c = 128 * h + 16 * b
         lz = act(T.lz[:, c:c + 16], T.zf[:, 16 * h:16 * h + 16], 0.0, T.ind4[:, bb:bb + 1])
-    need("s", t, su)
-    lin(cf(2), row(R_ONE), cf(0), 1.0 - ROUND / 2048)
-    lin(cf(3), row(R_ONE), cf(1), -2048.0)
-    lin(cf(4), row(R_ONE), cf(8), 6144.0)
-    lin(cf(9), row(R_ONE), row(R_F), 1.0)
-    t = lin(cf(10), row(R_ONE), cf(8), 4096.0)
+    need("s", t)
+    t = lin(cf(9), row(R_F), cf(1), 1.0)
+    for i, x in enumerate((cf(8), cf(0), cf(1))):
+        r1 = act(T.r1[:, 8 * i:8 * i + 8], grp, 0.0, x)
 
     for s in range(4):
         dlo = dma("y", T.lor[:, 128 * s:128 * s + 128], T.lob[32 * s:32 * s + 32, :], "dlo", lob)
-    dsa = dma("y", T.win[R_SLOT:128:16, :], T.sa[:, :], "dsa", wf, sa)
+    need("t", cst)
+    pc = P(te.matmul(T.psa[:, 0:24], T.onef[0:1, :], T.con[0:1, :], True, False))
     need("t", dlo, e8)
     plo = P(te.matmul(T.psl[:, :], T.e8[0:8, :], T.lor[:, :], True, True))
     need("t", lz, i3)
     te.matmul(T.psb[:, 0:32], T.lz[:, 0:128], T.i32f[:, :], True, False)
     pz = P(te.matmul(T.psb[:, 0:32], T.lz[:, 128:256], T.i32f[:, :], False, True))
-    need("v", plo, qs)
-    selm = ts(T.selm[:, :], T.psl[:, :], T.qs[:, 0:1], None, A.is_equal)
+    need("v", plo, qh)
+    selm = ts(T.selm[:, :], T.psl[:, :], cf(12), None, A.is_equal)
     need("v", pz)
     offm = copy(T.offm[:, :], T.psb[:, 0:32])
+    need("v", il, lane)
+    lt = ts(T.lt[:, :], T.il[:, :], cf(13), None, A.is_gt)
 
     need("s", a0, own0)
     dst = dma("y", T.c0[:, :], T.land0[:, 0:16, :], "dst", a0, own0)
     for b in range(4):
         dpb = dma("s", T.poolw[16 * b:16 * b + 16, :], T.land0[:, 16:80, :], "dpb")
         dpa = dma("y", T.poolw[16 * b + 64:16 * b + 80, :], T.land0[:, 16:80, :], "dpa")
-    dwa = dma("y", T.win[R_F:128:16, :], T.land1[:, :, :], "dwa", a1, own1)
+    dwa = dma("y", T.win[R_F:128:16, :], T.land1[:, :, :], "dwa", a1, own1, wf)
     dwb = dma("s", T.win[R_E:128:16, :], T.land1[:, :, :], "dwb", a1, own1, wf)
     dwq = dma("y", T.wq[:, :], T.land1[:, :, :], "dwq")
     need("s", t)
-    for i in range(3):
-        r1 = act(T.r1[:, 8 * i:8 * i + 8], grp, 0.0, cf(2 + i))
-    for i, x in enumerate((cf(9), cf(1), cf(10), row(R_SYM))):
-        r2f = act(T.r2f[:, 8 * i:8 * i + 8], grp, 0.0, x)
-    need("v", r2f)
-    r2 = copy(T.r2[:, :], T.r2f[:, :])
+    t = act(cf(10), cf(9), 0.0, 256.0)
+    act(T.r2[:, 0:8], grp, 0.0, cf(9))
+    pcf = lin(cf(18), qf, cf(17), 16.0)
+    need("s", t)
+    r2 = act(T.r2[:, 8:16], grp, 0.0, cf(10))
 
     gby, kept, bank = {}, {}, [None] * 4
 
@@ -256,31 +256,21 @@ def rank_program(g, core, T, topo):
         gby[s] = tt(T.gby[:, 128 * s:128 * s + 128], T.poolw[:, :].indirect(T.offm[:, 8 * s:8 * s + 8]),
                     T.selm[:, 128 * s:128 * s + 128], A.mult)
 
-    def segment(s, b0, n, i):
+    def segment(s, i):
         need("t", gby[s], se, *([bank[i]] if bank[i] else []))
-        for k in range(n):
-            p = P(te.matmul(T["ps%d" % i][:, 128 * k:128 * k + 128], T.selw[:, 128 * (b0 + k):128 * (b0 + k + 1)],
-                            T.gby[:, 128 * s:128 * s + 128], True, True))
-        return s, b0, n, i, p
+        for h in (0, 128):
+            p = P(te.matmul(T["ps%d" % i][:, h:h + 128], T.selw[32 * i:32 * i + 32, h:h + 128],
+                            T.gby[32 * i:32 * i + 32, 128 * s:128 * s + 128], True, True))
+        return s, i, p
 
-    def keep(s, b0, n, i, p):
+    def keep(s, i, p):
         need("s", p)
-        t = 1 + 1024 * s + 128 * b0
-        kept[s] = bank[i] = act(T.bw[:, t:t + 128 * n], T["ps%d" % i][:, 0:128 * n])
+        t = 1 + 1024 * s + 256 * i
+        kept[s] = bank[i] = act(T.bw[:, t:t + 256], T["ps%d" % i][:, 0:256])
 
-    def look(s):
-        return copy(T.ent[:, 128 * s:128 * s + 128], T.win[:, :].indirect(T.off[:, 8 * s:8 * s + 8]))
-
-    def letters(s, *toks):
-        need("t", *toks)
-        for c in range(8):
-            p = P(te.matmul(T.psl[0:8, 128 * s + c:128 * s + 128:8], T.r2[:, 24:32],
-                            T.ent[:, 128 * s + 16 * c:128 * s + 16 * c + 16], True, True))
-        return p
-
-    def symbols(s0, s1, p):
-        need("s", p)
-        return act(T.outs[:, 128 * s0:128 * s1], T.psl[0:8, 128 * s0:128 * s1])
+    def letters(s, tok):
+        need("s", tok, permo)
+        return act(T.outs[:, 128 * s:128 * s + 128], T.ent[:, 128 * s:128 * s + 128].indirect(T.permo[:, :]))
 
     def spread(out, tile):
         return tt(out[:, :], tile[:, :].indirect(T.clist[:, :]), T.maskf[:, :], A.mult)
@@ -296,57 +286,82 @@ def rank_program(g, core, T, topo):
     ph = P(te.matmul(T.psc[:, 0:8], T.sph[:, :], T.grh[:, :], True, True))
     need("v", dpa, dpb, offm, selm)
     gather(0)
-    keep(*segment(0, 0, 2, 0))
-    keep(*segment(0, 2, 2, 1))
-    need("v", ph)
-    h2 = ts(T.h2[:, :], T.psc[:, 0:8], 2048.0, None, A.add)
+    keep(*segment(0, 0))
 
+    W = T.w[:, 8:16]
     for s in range(4):
         c = 8 * s
+        E, look = T.ent[:, 128 * s:128 * s + 128], T.win[:, :].indirect(T.off[:, c:c + 8])
         if s == 0:
-            need("v", off, rnd, dwa, dwb, dsa)
-            ent = ts(T.ent0[:, :], T.win[:, :].indirect(T.off[:, 0:8]), cf(5), cf(6), A.add, A.add)
-            need("t", ent, r1)
-            pe = P(te.matmul(T.psa[:, 0:24], T.ent0[:, :], T.r1[:, :], True, True))
+            need("v", off, rnd, dwa, dwb)
+            ent = ts(E, look, cf(5), cf(6), A.add, A.add)
+            need("t", pc, ent, r1)
+            pe = P(te.matmul(T.psa[:, 0:24], E, T.r1[:, :], False, True))
             dlw = dma("y", T.win[R_SYM:128:16, :], T.land3[:, :, :], "dlw", a3, own3, ent)
-            keep(*segment(0, 4, 2, 2))
-            keep(*segment(0, 6, 2, 3))
+            for i in (1, 2, 3):
+                keep(*segment(0, i))
+            need("v", ph)
+            h2 = ts(T.h2[:, :], T.psc[:, 0:8], 2048.0, None, A.add)
             need("v", dwq)
-            ts(T.tb[:, 0:128], T.wq[:, :], 11, None, A.arith_shift_right)
-            t = ts(T.tb[:, 128:256], T.wq[:, :], 2047, None, A.bitwise_and)
+            t = ts(T.tb[:, 0:128], T.wq[:, :], 2.0 ** -11, 0.500244140625, A.mult, A.add)
             dma("y", T.win[R_F:128:16, :], T.tb[:, 0:128], "dtb", t)
-            dtb = dma("y", T.win[R_E:128:16, :], T.tb[:, 128:256], "dtb")
-            gather(1)
+            t = ts(T.tb[:, 128:256], T.wq[:, :], 2047, None, A.bitwise_and)
+            dtb = dma("y", T.win[R_E:128:16, :], T.tb[:, 128:256], "dtb", t)
+            need("v", pe, h2)
+            pr = tt(T.pr[:, :], T.psa[:, 8:16], T.h2[:, :], A.mult)
+            need("v", pcf)
+            permo = ts(T.permo[:, :], T.is1[:, 0:8], 2.0, cf(18), A.mult, A.add)
+            need("v", pr)
+            w = tt(W, T.pr[:, :], T.psa[:, 0:8], A.is_lt)
+            xq = tt(T.xq[:, :], T.pr[:, :], T.psa[:, 16:24], A.add)
+            need("v", w)
+            wc = V(v.tensor_tensor_scan(T.wc[:, 1:9], W, T.zer[:, :], T.wc[:, 0:1], A.add, A.add))
+            z = ts(T.z[:, :], W, 255.0, 1.0, A.mult, A.add)
+            X = T.xq[:, :]
         else:
-            need("v", off, dlw, dtb)
-            ent = look(s)
+            need("v", off, dlw, dtb, hr)
+            ent = tt(E, look, T.hr[:, :], A.mult)
             need("t", ent, r2)
-            pe = P(te.matmul(T.psa[:, 0:24], T.ent[:, 128 * s:128 * s + 128], T.r2[:, 0:24], True, True))
+            pe = P(te.matmul(T.psa[:, 0:16], E, T.r2[:, 0:16], True, True))
+            sym = letters(s, ent)
             if s == 1:
-                gather(3)
-                letters(1, selm)
+                gather(2)
+                keep(*segment(1, 2))
             elif s == 2:
-                sym = symbols(0, 3, letters(2))
-            else:
-                sym = symbols(3, 4, letters(3, sym))
-        need("v", pe, h2)
-        pr = tt(T.pr[:, :], T.psa[:, 0:8], T.h2[:, :], A.mult)
-        need("v", pr)
-        w = tt(T.w[:, :], T.pr[:, :], T.psa[:, 16:24], A.is_lt)
-        xq = tt(T.xq[:, :], T.pr[:, :], T.psa[:, 8:16], A.add)
-        need("v", w, con)
-        wc = V(v.tensor_tensor_scan(T.wc[:, c + 1:c + 9], T.w[:, :], T.zer[:, :], T.wc[:, c:c + 1], A.add, A.add))
-        g256 = ts(T.g256[:, :], T.w[:, :], 255.0, 1.0, A.mult, A.add)
-        need("t", w, lt, idn)
-        te.matmul(T.psb[:, 0:8], T.lt[:, :], T.w[:, :], True, False)
-        te.matmul(T.psb[:, 0:8], T.idn[:, :], T.w[:, :], False, False)
-        need("t", wc)
-        cn = P(te.matmul(T.psb[:, 0:8], T.ones[:, :], T.wc[:, c:c + 8], False, True))
-        need("v", g256)
-        y = tt(T.y[:, :], T.xq[:, :], T.g256[:, :], A.mult)
+                letters(0, copy(T.ent[:, 0:128], T.win[:, :].indirect(T.off[:, 0:8])))
+            keep(*segment(s, 3))
+            need("v", pe)
+            w = ts(W, T.psa[:, 0:8], 4096.0, None, A.is_lt)
+            z = ts(T.z[:, :], T.psa[:, 0:8], 4096.0, 1.0 / 256, A.is_lt, A.max)
+            if not SHIFTS:
+                need("v", w)
+                wc = V(v.tensor_tensor_scan(T.wc[:, c + 1:c + 9], W, T.zer[:, :], T.wc[:, c:c + 1], A.add, A.add))
+            X = T.psa[:, 8:16]
+        if SHIFTS and s > 0:
+            need("t", tot)
+            te.matmul(T.psb[:, 0:8], T.ones[:, :], T.tot[:, :], True, False)
+            need("t", w)
+            for d in range(1, 8):
+                te.matmul(T.psb[:, 0:8], T.ones[:, :], T.w[:, 8 - d:16 - d], False, False)
+            te.matmul(T.psb[:, 0:8], T.lt[:, :], W, False, False)
+            cn = P(te.matmul(T.psb[:, 0:8], T.idn[:, :], W, False, True))
+        else:
+            need("t", w, lt, idn)
+            te.matmul(T.psb[:, 0:8], T.lt[:, :], W, True, False)
+            te.matmul(T.psb[:, 0:8], T.idn[:, :], W, False, False)
+            need("t", wc)
+            cn = P(te.matmul(T.psb[:, 0:8], T.ones[:, :], T.wc[:, c:c + 8], False, True))
+        need("v", z)
+        y = tt(T.y[:, :], X, T.z[:, :], A.mult)
+        if SHIFTS and 0 < s < 3:
+            wc = V(v.tensor_tensor_scan(T.wc[:, c + 1:c + 9], W, T.zer[:, :], T.wc[:, c:c + 1], A.add, A.add))
         if s < 3:
             need("v", y)
             ylo = ts(T.ylo[:, :], T.y[:, :], 2047, None, A.bitwise_and)
+            hx = ts(T.hx[:, R_F:128:16], T.y[:, :], 2.0 ** -11, 1023.500244140625, A.mult, A.add)
+        elif s == 3 and not SHIFTS:
+            need("v", y)
+            t = spread(T.spf, T.y)
         need("v", cn)
         off2 = ts(T.off2[:, c:c + 8], T.psb[:, 0:8], 1.0 - READS, None, A.add)
         need("s", off2, con, kept[s])
@@ -354,33 +369,41 @@ def rank_program(g, core, T, topo):
         if s < 3:
             need("v", ylo)
             t = spread(T.sph, T.ylo)
-            h2 = ts(T.h2[:, :], T.y[:, :], 2.0 ** -11, -0.499755859375, A.mult, A.add)
-            p0 = segment(s + 1, 0, 4, 2 * (s % 2))
+            if SHIFTS:
+                tot = ts(T.tot[:, :], T.zer[:, :], T.wc[:, c + 8:c + 9], None, A.add)
+            if s > 0:
+                p0 = segment(s + 1, 0)
+            need("t", hx, off2)
+            pr_ = P(te.matmul(T.psb[:, 128:256], T.hx[:, :], T.idn[:, :], True, True))
             need("t", t)
             te.matmul(T.psc[:, 0:8], T.sph[:, :], T.grh[:, :], True, False)
         else:
-            need("v", y)
-            t = spread(T.spf, T.y)
+            if SHIFTS:
+                need("v", y)
+                t = spread(T.spf, T.y)
             need("t", t)
             te.matmul(T.psc[:, 0:8], T.spf[:, :], grp, True, False)
         need("t", gb, r3)
         pb = P(te.matmul(T.psc[:, 0:8], T.gb[:, :], T.r3[:, :], False, True))
         if s == 0:
-            gather(2)
+            gather(1)
+            p0 = segment(1, 0)
         elif s == 1:
-            late = look(0)
+            gather(3)
         need("v", pb)
         if s == 3:
             xl = copy(T.xl[:, :], T.psc[:, 0:8])
             break
         off = copy(T.off[:, c + 8:c + 16], T.psc[:, 0:8])
+        need("s", pr_)
+        hr = lin(T.hr[:, :], T.psb[:, 128:256], cf(16), 1.0 / READS)
         keep(*p0)
-        keep(*segment(s + 1, 4, 4, 2 * (s % 2) + 1))
-        if s == 1:
-            letters(0, late)
+        keep(*segment(s + 1, 1))
+        if s > 0:
+            keep(*segment(s + 1, 2))
 
-    dsy = dma("y", T.snd4[:, :, :], T.outs[:, :], "dsy", sym)
-    dow4 = dma("y", T.land4[me, :, :], T.outs[me:me + 1, :], "dow4")
+    dsy = dma("y", T.snd4[:, :, :], T.outs[R_SYM:128:16, :], "dsy", sym)
+    dow4 = dma("y", T.land4[me, :, :], T.outs[16 * me + R_SYM:16 * me + R_SYM + 1, :], "dow4")
     need("g", dsy)
     a4 = send(T.snd4, T.land4, "a4")
     dla = dma("y", T.snd5[:, :, :], T.xl[:, :], "dla", xl)

@@ -6,14 +6,14 @@ SCRATCH = {}
 for _i, _w, _t in ((0, 8, I32), (1, 16, I32), (3, 16, I32), (4, 4, F32), (5, 1, F32)):
     SCRATCH["snd%d" % _i] = SCRATCH["land%d" % _i] = ("dram", [8, 128, _w], _t)
 for _t, _l in (
-        (I32, "ij 128 is1 128 il 128 ip 8 pi 8"
-              " pl 32 zz 32 zh 32 loi 32 poolw 256 win 2048 c0 8 h0 8 h2 8 y 8 ylo 8 sl 8 wq 128 tb 256"),
-        (U16, "clist 8 permo 8 offm 32 off 32 off2 32"),
-        (F32, "pf 8 cf 24 maskf 128 grp 8 zf 32 lh 32 ind4 4 r1 24 r2 16 ent 512 onef 128 con 24 pr 8 xq 8 z 8 xl 8"
+        (I32, "i8 64 ij 128 is1 128 il 128 ip 8 pi 8"
+              " pl 32 zz 32 zh 32 loi 32 poolw 256 win 2048 c0 8 h0 8 h2 16 y 16 ylo 8 sl 8 wq 128 tb 256"),
+        (U16, "clist 16 permo 8 offm 32 off 32 off2 32"),
+        (F32, "pf 8 cf 24 maskf 128 grp 8 zf 32 lh 32 ind4 4 r1 40 r2 16 ent 512 onef 128 con 40 pr 16 xq 16 lift 16 xl 8"
               " spf 128 hr 128 outs 512"),
         (F16, "sph 128 grh 8 hx 128"),
-        (B16, "lt 128 idn 128 big 128 e8 128 ones 128 selw 256 zer 8 r3 8 lob 32 selm 512 gby 512 bw 4112 w 16 wc 48 gb 128"
-              " lz 256 i32f 32 tot 8")):
+        (B16, "lt 128 idn 128 big 128 e8 128 ones 128 selw 256 zer 8 r3 16 lob 32 selm 512 gby 512 bw 4112 w 144 wc 48 gb 128"
+              " lz 256 i32f 32 gt 128 idk 128 ma 128 mb 128 s64 64 seg 384")):
     _l = _l.split()
     for _i in range(0, len(_l), 2):
         SCRATCH[_l[_i]] = ("sbuf", [128, int(_l[_i + 1])], _t)
@@ -22,10 +22,11 @@ for _i in ("ps0", "ps1", "ps2", "ps3", "psl", "psa", "psb", "psc"):
     SCRATCH[_i] = ("psum", [128, 512], F32)
 SEMAPHORES = ["gi", "v", "t", "s", "ls", "a0", "a1", "a3", "a4", "a5", "l3", "dtb", "dlw",
               "l0", "l1", "own0", "own1", "own3", "lpl", "lzz", "dlo", "dst", "dpa",
-              "dpb", "dwa", "dwb", "dwq", "dsy", "dow4", "dla", "dow5", "fsy", "fla"]
+              "dpb", "dwa", "dwb", "dwq", "dsy", "dow4", "dla", "dow5", "fsy", "fla", "dk1", "dk2", "dk3"]
 ROUND = 1.5 * 2.0 ** 34
 READS = 8192.0
-SHIFTS = False
+LIFT = 255.0 * 4096
+B0 = 16
 R_F, R_E, R_SLOT, R_SYM = 0, 1, 2, 3
 
 
@@ -68,6 +69,9 @@ def rank_program(g, core, T, topo):
 
     def tt(out, a, b, op):
         return V(v.tensor_tensor(out, a, b, op))
+
+    def scan(out, a, b, first, o1, o2):
+        return V(v.tensor_tensor_scan(out, a, b, first, o1, o2))
 
     def copy(out, in_):
         return V(v.tensor_copy(out, in_))
@@ -135,6 +139,7 @@ def rank_program(g, core, T, topo):
     need("g", l3)
     a3 = send(T.snd3, T.land3, "a3")
     il = pattern(T.il[:, :], [[1, 8], [8, 16]], 0, 0)
+    i8 = pattern(T.i8[:, :], [[0, 8], [1, 8]], 0, 0)
     idn = did(g.affine_select(T.idn[:, :], T.big[:, :], [[-1, 128]], A.is_equal, 0.0, 0, 1), "gi")
 
     def row(a):
@@ -152,13 +157,17 @@ def rank_program(g, core, T, topo):
 
     fill(T.lz[:, :], 0.0)
     fill(T.zer[:, :], 0.0)
-    fill(T.wc[:, 0:1], 0.0)
-    con = fill(T.bw[:, 0:1], 0.0)
+    fill(T.wc[:, :], 0.0)
+    fill(T.w[:, :], 0.0)
+    fill(T.lift[:, 0:16:2], 2.0 ** 30)
+    fill(T.lift[:, 1:16:2], -LIFT)
+    con = fill(T.bw[:, 0:B0], 0.0)
     hx = fill(T.hx[:, :], 1.0)
     need("s", ones)
     act(T.onef[0:1, :], T.ones[0:1, :])
-    for i, x in enumerate((6144.0, 1.0 - ROUND / 2048, -2048.0)):
-        cst = act(T.con[0:1, 8 * i:8 * i + 8], T.ones[0:1, 0:8], 0.0, x)
+    cols = (slice(0, 8), slice(8, 24, 2), slice(9, 24, 2), slice(24, 40, 2), slice(25, 40, 2))
+    for i, x in zip(cols, (6144.0, 256.0 - ROUND / 8, 1.0 - ROUND / 2048, -2048.0 * 256, -2048.0)):
+        cst = act(T.con[0:1, i], T.ones[0:1, 0:8], 0.0, x)
     need("v", is1)
     ts(T.ij[:, :], T.is1[:, :], 15, None, A.bitwise_and)
     need("v", ip)
@@ -195,34 +204,52 @@ def rank_program(g, core, T, topo):
     i3 = ts(T.i32f[:, :], T.is1[:, 0:32], cf(7), None, A.is_equal)
     wf = slots(9, 16)
     grh = copy(T.grh[:, :], grp)
-    clist = copy(T.clist[:, :], T.is1[:, 0:8])
+    copy(T.clist[:, 0:8], T.is1[:, 0:8])
+    clist = copy(T.clist[:, 8:16], T.is1[:, 1:16:2])
+    need("v", il, lane)
+    lt = ts(T.lt[:, :], T.il[:, :], cf(13), None, A.is_gt)
+    gt = ts(T.gt[:, :], T.il[:, :], cf(13), None, A.is_lt)
+    need("v", i8)
+    s64 = ts(T.s64[:, :], T.i8[:, :], T.pf[:, 1:2], None, A.is_equal)
+    need("g", lt)
+    ma = did(g.affine_select(T.ma[:, :], T.lt[:, :], [[-1, 128]], A.not_equal, READS, 0, 1), "gi")
+    need("g", gt)
+    mb = did(g.affine_select(T.mb[:, :], T.gt[:, :], [[-1, 128]], A.not_equal, -READS, 0, 1), "gi")
+    bwf = {s: did(g.iota(T.bw[:, B0 + 1024 * s:B0 + 1024 * s + 1024], [[0, 1024]], 1, 0,
+                         allow_small_or_imprecise_dtypes=True), "gi") for s in (1, 2, 3)}
 
     need("s", mf)
     act(cf(0), row(R_F), 0.0, 2.0 ** -11)
     act(cf(14), row(R_E), 0.0, -1.0)
     t = act(cf(15), row(R_SLOT), 0.0, -1.0)
     act(cf(5), row(R_F), 0.0, -1023.5)
-    act(cf(16), row(R_F), 0.0, -1024.0)
+    act(cf(16), row(R_F), 0.0, -1534.0)
+    act(cf(2), row(R_F), 0.0, 2.0 ** -3)
     rnd = act(cf(6), row(R_F), 0.0, ROUND)
     need("s", t)
     se = lin(T.selw[:, 0:128], T.selw[:, 128:256], 1.0, -1.0)
     lin(cf(1), row(R_SLOT), cf(14), 1.0)
+    lin(cf(4), row(1), row(0), LIFT)
     t = lin(cf(8), row(R_E), cf(15), 1.0)
-    r3 = act(T.r3[:, :], grp, 0.0, 1.0 / 16)
+    act(T.r3[:, 0:8], grp, 0.0, row(0))
     need("s", zf)
     for b in range(8):
         h, bb = b // 4, b % 4
         c = 128 * h + 16 * b
         lz = act(T.lz[:, c:c + 16], T.zf[:, 16 * h:16 * h + 16], 0.0, T.ind4[:, bb:bb + 1])
     need("s", t)
-    t = lin(cf(9), row(R_F), cf(1), 1.0)
-    for i, x in enumerate((cf(8), cf(0), cf(1))):
-        r1 = act(T.r1[:, 8 * i:8 * i + 8], grp, 0.0, x)
+    r3 = act(T.r3[:, 8:16], grp, 0.0, cf(4))
+    lin(cf(9), row(R_F), cf(1), 1.0)
+    t = act(cf(3), cf(1), 0.0, 256.0)
+    for i, x in zip(cols, (cf(8), cf(2), cf(0), cf(3), cf(1))):
+        if i == cols[3]:
+            need("s", t)
+        r1 = act(T.r1[:, i], grp, 0.0, x)
 
     for s in range(4):
         dlo = dma("y", T.lor[:, 128 * s:128 * s + 128], T.lob[32 * s:32 * s + 32, :], "dlo", lob)
     need("t", cst)
-    pc = P(te.matmul(T.psa[:, 0:24], T.onef[0:1, :], T.con[0:1, :], True, False))
+    pc = P(te.matmul(T.psa[:, 0:40], T.onef[0:1, :], T.con[0:1, :], True, False))
     need("t", dlo, e8)
     plo = P(te.matmul(T.psl[:, :], T.e8[0:8, :], T.lor[:, :], True, True))
     need("t", lz, i3)
@@ -232,8 +259,6 @@ def rank_program(g, core, T, topo):
     selm = ts(T.selm[:, :], T.psl[:, :], cf(12), None, A.is_equal)
     need("v", pz)
     offm = copy(T.offm[:, :], T.psb[:, 0:32])
-    need("v", il, lane)
-    lt = ts(T.lt[:, :], T.il[:, :], cf(13), None, A.is_gt)
 
     need("s", a0, own0)
     dst = dma("y", T.c0[:, :], T.land0[:, 0:16, :], "dst", a0, own0)
@@ -245,10 +270,11 @@ def rank_program(g, core, T, topo):
     dwq = dma("y", T.wq[:, :], T.land1[:, :, :], "dwq")
     need("s", t)
     t = act(cf(10), cf(9), 0.0, 256.0)
-    act(T.r2[:, 0:8], grp, 0.0, cf(9))
+    act(T.r2[:, 1:16:2], grp, 0.0, cf(9))
     pcf = lin(cf(18), qf, cf(17), 16.0)
-    need("s", t)
-    r2 = act(T.r2[:, 8:16], grp, 0.0, cf(10))
+    need("s", t, idn)
+    r2 = act(T.r2[:, 0:16:2], grp, 0.0, cf(10))
+    idk = act(T.idk[:, :], T.idn[:, :], 0.0, LIFT / 2048)
 
     gby, kept, bank = {}, {}, [None] * 4
 
@@ -256,24 +282,29 @@ def rank_program(g, core, T, topo):
         gby[s] = tt(T.gby[:, 128 * s:128 * s + 128], T.poolw[:, :].indirect(T.offm[:, 8 * s:8 * s + 8]),
                     T.selm[:, 128 * s:128 * s + 128], A.mult)
 
-    def segment(s, i):
-        need("t", gby[s], se, *([bank[i]] if bank[i] else []))
+    def segment(i):
+        need("t", gby[0], se)
         for h in (0, 128):
             p = P(te.matmul(T["ps%d" % i][:, h:h + 128], T.selw[32 * i:32 * i + 32, h:h + 128],
-                            T.gby[32 * i:32 * i + 32, 128 * s:128 * s + 128], True, True))
-        return s, i, p
-
-    def keep(s, i, p):
+                            T.gby[32 * i:32 * i + 32, 0:128], True, True))
         need("s", p)
-        t = 1 + 1024 * s + 256 * i
-        kept[s] = bank[i] = act(T.bw[:, t:t + 256], T["ps%d" % i][:, 0:256])
+        t = B0 + 256 * i
+        kept[0] = bank[i] = lin(T.bw[:, t:t + 256], T["ps%d" % i][:, 0:256], row(1), row(0))
+
+    def thousand(s):
+        a, ps = 128 * s - 128, T["ps%d" % (s - 1)][0:64, 0:128]
+        need("t", gby[s], s64, bank[s - 1])
+        p = P(te.matmul(ps, T.s64[:, :], T.gby[:, 128 * s:128 * s + 128], True, True))
+        need("s", p)
+        t = act(T.seg[0:64, a:a + 128], ps)
+        kept[s] = dma("y", T.bw[0:128:16, B0 + 1024 * s:B0 + 1024 * s + 1024], T.seg[0:64, a:a + 128], "dk%d" % s, t, bwf[s])
 
     def letters(s, tok):
         need("s", tok, permo)
         return act(T.outs[:, 128 * s:128 * s + 128], T.ent[:, 128 * s:128 * s + 128].indirect(T.permo[:, :]))
 
     def spread(out, tile):
-        return tt(out[:, :], tile[:, :].indirect(T.clist[:, :]), T.maskf[:, :], A.mult)
+        return tt(out[:, :], tile[:, :].indirect(T.clist[:, 0:8]), T.maskf[:, :], A.mult)
 
     need("v", dst)
     sl = ts(T.sl[:, :], T.c0[:, :], 2047, None, A.bitwise_and)
@@ -286,9 +317,10 @@ def rank_program(g, core, T, topo):
     ph = P(te.matmul(T.psc[:, 0:8], T.sph[:, :], T.grh[:, :], True, True))
     need("v", dpa, dpb, offm, selm)
     gather(0)
-    keep(*segment(0, 0))
+    segment(0)
 
-    W = T.w[:, 8:16]
+    W, WB = T.w[:, 16:144:16], T.w[:, 0:128:16]
+    Y = T.y[:, 1:16:2]
     for s in range(4):
         c = 8 * s
         E, look = T.ent[:, 128 * s:128 * s + 128], T.win[:, :].indirect(T.off[:, c:c + 8])
@@ -296,111 +328,83 @@ def rank_program(g, core, T, topo):
             need("v", off, rnd, dwa, dwb)
             ent = ts(E, look, cf(5), cf(6), A.add, A.add)
             need("t", pc, ent, r1)
-            pe = P(te.matmul(T.psa[:, 0:24], E, T.r1[:, :], False, True))
+            pe = P(te.matmul(T.psa[:, 0:40], E, T.r1[:, :], False, True))
             dlw = dma("y", T.win[R_SYM:128:16, :], T.land3[:, :, :], "dlw", a3, own3, ent)
             for i in (1, 2, 3):
-                keep(*segment(0, i))
+                segment(i)
             need("v", ph)
-            h2 = ts(T.h2[:, :], T.psc[:, 0:8], 2048.0, None, A.add)
+            for i in (0, 1):
+                h2 = ts(T.h2[:, i:16:2], T.psc[:, 0:8], 2048.0, None, A.add)
             need("v", dwq)
             t = ts(T.tb[:, 0:128], T.wq[:, :], 2.0 ** -11, 0.500244140625, A.mult, A.add)
             dma("y", T.win[R_F:128:16, :], T.tb[:, 0:128], "dtb", t)
             t = ts(T.tb[:, 128:256], T.wq[:, :], 2047, None, A.bitwise_and)
             dtb = dma("y", T.win[R_E:128:16, :], T.tb[:, 128:256], "dtb", t)
             need("v", pe, h2)
-            pr = tt(T.pr[:, :], T.psa[:, 8:16], T.h2[:, :], A.mult)
+            pr = tt(T.pr[:, :], T.psa[:, 8:24], T.h2[:, :], A.mult)
             need("v", pcf)
             permo = ts(T.permo[:, :], T.is1[:, 0:8], 2.0, cf(18), A.mult, A.add)
             need("v", pr)
-            w = tt(W, T.pr[:, :], T.psa[:, 0:8], A.is_lt)
-            xq = tt(T.xq[:, :], T.pr[:, :], T.psa[:, 16:24], A.add)
-            need("v", w)
-            wc = V(v.tensor_tensor_scan(T.wc[:, 1:9], W, T.zer[:, :], T.wc[:, 0:1], A.add, A.add))
-            z = ts(T.z[:, :], W, 255.0, 1.0, A.mult, A.add)
+            w = tt(W, T.pr[:, 1:16:2], T.psa[:, 0:8], A.is_lt)
+            xq = tt(T.xq[:, :], T.pr[:, :], T.psa[:, 24:40], A.add)
+            need("v", xq)
             X = T.xq[:, :]
         else:
+            need("t", wc)
+            te.matmul(T.psb[:, 0:8], T.ones[:, :], T.wc[:, 2 * c - 9:2 * c - 1], True, False)
             need("v", off, dlw, dtb, hr)
             ent = tt(E, look, T.hr[:, :], A.mult)
             need("t", ent, r2)
             pe = P(te.matmul(T.psa[:, 0:16], E, T.r2[:, 0:16], True, True))
             sym = letters(s, ent)
-            if s == 1:
-                gather(2)
-                keep(*segment(1, 2))
-            elif s == 2:
-                letters(0, copy(T.ent[:, 0:128], T.win[:, :].indirect(T.off[:, 0:8])))
-            keep(*segment(s, 3))
+            if s < 3:
+                gather(s + 1)
+                thousand(s + 1)
+            else:
+                sym = letters(0, copy(T.ent[:, 0:128], T.win[:, :].indirect(T.off[:, 0:8])))
             need("v", pe)
-            w = ts(W, T.psa[:, 0:8], 4096.0, None, A.is_lt)
-            z = ts(T.z[:, :], T.psa[:, 0:8], 4096.0, 1.0 / 256, A.is_lt, A.max)
-            if not SHIFTS:
-                need("v", w)
-                wc = V(v.tensor_tensor_scan(T.wc[:, c + 1:c + 9], W, T.zer[:, :], T.wc[:, c:c + 1], A.add, A.add))
-            X = T.psa[:, 8:16]
-        if SHIFTS and s > 0:
-            need("t", tot)
-            te.matmul(T.psb[:, 0:8], T.ones[:, :], T.tot[:, :], True, False)
-            need("t", w)
-            for d in range(1, 8):
-                te.matmul(T.psb[:, 0:8], T.ones[:, :], T.w[:, 8 - d:16 - d], False, False)
-            te.matmul(T.psb[:, 0:8], T.lt[:, :], W, False, False)
-            cn = P(te.matmul(T.psb[:, 0:8], T.idn[:, :], W, False, True))
-        else:
-            need("t", w, lt, idn)
-            te.matmul(T.psb[:, 0:8], T.lt[:, :], W, True, False)
-            te.matmul(T.psb[:, 0:8], T.idn[:, :], W, False, False)
-            need("t", wc)
-            cn = P(te.matmul(T.psb[:, 0:8], T.ones[:, :], T.wc[:, c:c + 8], False, True))
-        need("v", z)
-        y = tt(T.y[:, :], X, T.z[:, :], A.mult)
-        if SHIFTS and 0 < s < 3:
-            wc = V(v.tensor_tensor_scan(T.wc[:, c + 1:c + 9], W, T.zer[:, :], T.wc[:, c:c + 1], A.add, A.add))
+            w = ts(W, T.psa[:, 1:16:2], 4096.0, None, A.is_lt)
+            X = T.psa[:, 0:16]
+        y = scan(T.y[:, :], T.lift[:, :], X, 0.0, A.add, A.min)
+        need("t", w, ma, mb)
+        te.matmul(T.psb[:, 0:8], T.ma[:, :], W, s == 0, False)
+        cn = P(te.matmul(T.psb[:, 0:8], T.mb[:, :], WB, False, True))
+        need("v", y)
         if s < 3:
-            need("v", y)
-            ylo = ts(T.ylo[:, :], T.y[:, :], 2047, None, A.bitwise_and)
-            hx = ts(T.hx[:, R_F:128:16], T.y[:, :], 2.0 ** -11, 1023.500244140625, A.mult, A.add)
-        elif s == 3 and not SHIFTS:
-            need("v", y)
-            t = spread(T.spf, T.y)
+            ylo = ts(T.ylo[:, :], Y, 2047, None, A.bitwise_and)
+            hx = ts(T.hx[:, R_F:128:16], Y, 2.0 ** -11, 1533.500244140625, A.mult, A.add)
+            need("t", idk, selm)
+            te.matmul(T.psl[:, 0:128], T.w[:, 16:144], T.idk[:, :], True, False)
+            need("t", hx, idn)
+            pr_ = P(te.matmul(T.psl[:, 0:128], T.hx[:, :], T.idn[:, :], False, True))
+        else:
+            t = tt(T.spf[:, :], T.y[:, :].indirect(T.clist[:, 8:16]), T.maskf[:, :], A.mult)
         need("v", cn)
-        off2 = ts(T.off2[:, c:c + 8], T.psb[:, 0:8], 1.0 - READS, None, A.add)
+        off2 = scan(T.off2[:, c:c + 8], T.psb[:, 0:8], WB, B0 - READS, A.add, A.add)
         need("s", off2, con, kept[s])
-        gb = act(T.gb[:, :], T.bw[:, 0:1025 + 1024 * s].indirect(T.off2[:, c:c + 8]))
+        gb = act(T.gb[:, :], T.bw[:, 0:B0 + 1024 + 1024 * s].indirect(T.off2[:, c:c + 8]))
         if s < 3:
             need("v", ylo)
             t = spread(T.sph, T.ylo)
-            if SHIFTS:
-                tot = ts(T.tot[:, :], T.zer[:, :], T.wc[:, c + 8:c + 9], None, A.add)
-            if s > 0:
-                p0 = segment(s + 1, 0)
-            need("t", hx, off2)
-            pr_ = P(te.matmul(T.psb[:, 128:256], T.hx[:, :], T.idn[:, :], True, True))
+            wc = scan(T.wc[:, 2 * c:2 * c + 8], W, T.zer[:, :], T.wc[:, 2 * c - 9:2 * c - 8] if s else 0.0, A.add, A.add)
             need("t", t)
             te.matmul(T.psc[:, 0:8], T.sph[:, :], T.grh[:, :], True, False)
         else:
-            if SHIFTS:
-                need("v", y)
-                t = spread(T.spf, T.y)
             need("t", t)
             te.matmul(T.psc[:, 0:8], T.spf[:, :], grp, True, False)
         need("t", gb, r3)
-        pb = P(te.matmul(T.psc[:, 0:8], T.gb[:, :], T.r3[:, :], False, True))
+        pb = P(te.matmul(T.psc[:, 0:8], T.gb[:, :], T.r3[:, 0:8] if s < 3 else T.r3[:, 8:16], False, True))
         if s == 0:
             gather(1)
-            p0 = segment(1, 0)
-        elif s == 1:
-            gather(3)
         need("v", pb)
         if s == 3:
             xl = copy(T.xl[:, :], T.psc[:, 0:8])
             break
         off = copy(T.off[:, c + 8:c + 16], T.psc[:, 0:8])
         need("s", pr_)
-        hr = lin(T.hr[:, :], T.psb[:, 128:256], cf(16), 1.0 / READS)
-        keep(*p0)
-        keep(*segment(s + 1, 1))
-        if s > 0:
-            keep(*segment(s + 1, 2))
+        hr = lin(T.hr[:, :], T.psl[:, 0:128], cf(16), 1.0 / READS)
+        if s == 0:
+            thousand(1)
 
     dsy = dma("y", T.snd4[:, :, :], T.outs[R_SYM:128:16, :], "dsy", sym)
     dow4 = dma("y", T.land4[me, :, :], T.outs[16 * me + R_SYM:16 * me + R_SYM + 1, :], "dow4")

from concourse.bass import DstId, RemoteDMATransfer
from concourse.mybir import AluOpType as A, ActivationFunctionType as F

I32, U16, F32, B16, F16 = "int32", "uint16", "float32", "bfloat16", "float16"
SCRATCH = {}
for _i, _w, _t in ((0, 8, I32), (1, 16, I32), (3, 16, I32), (4, 4, F32), (5, 1, F32)):
    SCRATCH["snd%d" % _i] = SCRATCH["land%d" % _i] = ("dram", [8, 128, _w], _t)
for _t, _l in (
        (I32, "i8 64 ij 128 is1 128 il 128 ip 8 pi 8"
              " pl 32 zz 32 zh 32 loi 32 poolw 256 win 2048 c0 8 h0 8 h2 16 y 16 ylo 8 sl 8 wq 128 tb 256"),
        (U16, "clist 16 permo 8 offm 32 off 32 off2 32"),
        (F32, "pf 8 cf 24 maskf 128 grp 8 zf 32 lh 32 ind4 4 r1 40 r2 16 ent 512 onef 128 con 40 pr 16 xq 16 lift 16 xl 8"
              " spf 128 hr 128 outs 512"),
        (F16, "sph 128 grh 8 hx 128"),
        (B16, "lt 128 idn 128 big 128 e8 128 ones 128 selw 256 zer 8 r3 16 lob 32 selm 512 gby 512 bw 4112 w 144 wc 48 gb 128"
              " lz 256 i32f 32 gt 128 idk 128 ma 128 mb 128 s64 64 seg 384")):
    _l = _l.split()
    for _i in range(0, len(_l), 2):
        SCRATCH[_l[_i]] = ("sbuf", [128, int(_l[_i + 1])], _t)
SCRATCH["lor"] = ("sbuf", [8, 512], B16)
for _i in ("ps0", "ps1", "ps2", "ps3", "psl", "psa", "psb", "psc"):
    SCRATCH[_i] = ("psum", [128, 512], F32)
SEMAPHORES = ["gi", "v", "t", "s", "ls", "a0", "a1", "a3", "a4", "a5", "l3", "dtb", "dlw",
              "l0", "l1", "own0", "own1", "own3", "lpl", "lzz", "dlo", "dst", "dpa",
              "dpb", "dwa", "dwb", "dwq", "dsy", "dow4", "dla", "dow5", "fsy", "fla", "dk1", "dk2", "dk3"]
ROUND = 1.5 * 2.0 ** 34
READS = 8192.0
LIFT = 255.0 * 4096
B0 = 16
R_F, R_E, R_SLOT, R_SYM = 0, 1, 2, 3


def rank_program(g, core, T, topo):
    me = T.rank_of(core)
    if me is None:
        return
    Q = {"g": g, "v": g.vector, "s": g.scalar, "y": g.sync, "t": g.tensor}
    cnt, seen, waited = {}, {}, {}

    def did(ins, sem, n=1):
        ins.then_inc(T.sem[sem], n)
        cnt[sem] = cnt.get(sem, 0) + n
        return (sem, cnt[sem])

    def need(q, *toks):
        for sem, val in toks:
            if seen.get((q, sem), 0) < val:
                Q[q].wait_ge(T.sem[sem], val)
                seen[(q, sem)] = val
                waited[sem] = max(waited.get(sem, 0), val)

    v, ac, te = g.vector, g.scalar, g.tensor

    def dma(q, out, in_, sem, *toks):
        need(q, *toks)
        return did(Q[q].dma_start(out, in_), sem, 16)

    def V(ins):
        return did(ins, "v")

    def S(ins):
        return did(ins, "s")

    def P(ins):
        return did(ins, "t")

    def ts(out, in_, s1, s2, o1, *o2):
        return V(v.tensor_scalar(out, in_, s1, s2, o1, *o2))

    def tt(out, a, b, op):
        return V(v.tensor_tensor(out, a, b, op))

    def scan(out, a, b, first, o1, o2):
        return V(v.tensor_tensor_scan(out, a, b, first, o1, o2))

    def copy(out, in_):
        return V(v.tensor_copy(out, in_))

    def fill(ap, x):
        return V(v.memset(ap, x))

    def act(out, in_, *sc):
        return S(ac.activation(out, in_, F.Copy, *sc))

    def lin(out, in_, bias, scale):
        return S(ac.activation(out, in_, F.Identity, bias, scale))

    others = [d for d in T.cores if d != core]
    near = topo.cores_of(core)
    eng, k, kk = {}, 0, 0
    for d in others:
        es = topo.engines(core, d)
        if d in near:
            kk += 1
            eng[d] = es[-kk]
        else:
            eng[d] = (es[0::2] + es[1::2])[k]
            k += 1

    def send(src, dst, arr):
        tr = []
        for d in others:
            rid, pnc = topo.addr(d, core)
            tr.append(RemoteDMATransfer(dst_ids=[DstId(rid=rid, pnc=pnc)], dma_engine_mask=1 << eng[d],
                                        remote_sem=T.sem[arr], src=src[T.rank_of(d)], dst=dst[me]))
        g.remote_dma_fused(tr, local_sem=T.sem.ls)
        cnt["ls"] = cnt.get("ls", 0) + len(tr)
        cnt[arr] = len(others)
        return (arr, len(others))

    dma("s", T.snd0[:, 0:16, :], T.states[:, :], "l0")
    dma("y", T.snd0[:, 16:80, :], T.stock[:, :], "l0")
    l0 = dma("s", T.snd0[:, 80:128, :], T.models[:, 0:384], "l0")
    l1 = dma("y", T.snd1[:, :, :], T.models[:, :], "l1")
    lpl = dma("y", T.pl[:, :], T.places[me, :], "lpl")
    for s in range(4):
        for h in range(2):
            t = 1024 * s + 512 * h
            lzz = dma("s", T.zz[32 * s:32 * s + 32, 16 * h:16 * h + 16], T.places[me, t:t + 512], "lzz")
    l3 = dma("y", T.snd3[:, :, :], T.letters[:, :], "l3")
    dma("y", T.land0[me, 0:16, :], T.states[me, :], "own0")
    own0 = dma("y", T.land0[me, 16:80, :], T.stock[me, :], "own0")
    own1 = dma("y", T.land1[me, :, :], T.models[me, :], "own1")
    own3 = dma("y", T.land3[me, :, :], T.letters[me, :], "own3")

    def pattern(out, pat, base, mul):
        return did(g.iota(out, pat, base, mul), "gi")

    is1 = pattern(T.is1[:, :], [[1, 128]], 0, 0)
    ip = pattern(T.ip[:, 0:1], [[0, 1]], 0, 1)
    ones = fill(T.ones[:, :], 1.0)
    big = fill(T.big[:, :], READS)
    need("g", big)
    e8 = did(g.affine_select(T.e8[:, :], T.ones[:, :], [[-1, 8], [0, 16]], A.is_equal, 0.0, 0, 1), "gi")
    need("g", l0)
    a0 = send(T.snd0, T.land0, "a0")
    need("g", l1)
    a1 = send(T.snd1, T.land1, "a1")
    need("g", l3)
    a3 = send(T.snd3, T.land3, "a3")
    il = pattern(T.il[:, :], [[1, 8], [8, 16]], 0, 0)
    i8 = pattern(T.i8[:, :], [[0, 8], [1, 8]], 0, 0)
    idn = did(g.affine_select(T.idn[:, :], T.big[:, :], [[-1, 128]], A.is_equal, 0.0, 0, 1), "gi")

    def row(a):
        return T.maskf[:, a:a + 1]

    def cf(i):
        return T.cf[:, i:i + 1]

    grp = T.grp[:, :]

    def slots(k0, k1):
        for k in range(k0, k1):
            t = ts(T.win[:, 128 * k:128 * k + 128], T.is1[:, :], 128.0 * k, None, A.add)
        return t

    fill(T.lz[:, :], 0.0)
    fill(T.zer[:, :], 0.0)
    fill(T.wc[:, :], 0.0)
    fill(T.w[:, :], 0.0)
    fill(T.lift[:, 0:16:2], 2.0 ** 30)
    fill(T.lift[:, 1:16:2], -LIFT)
    con = fill(T.bw[:, 0:B0], 0.0)
    hx = fill(T.hx[:, :], 1.0)
    need("s", ones)
    act(T.onef[0:1, :], T.ones[0:1, :])
    cols = (slice(0, 8), slice(8, 24, 2), slice(9, 24, 2), slice(24, 40, 2), slice(25, 40, 2))
    for i, x in zip(cols, (6144.0, 256.0 - ROUND / 8, 1.0 - ROUND / 2048, -2048.0 * 256, -2048.0)):
        cst = act(T.con[0:1, i], T.ones[0:1, 0:8], 0.0, x)
    need("v", is1)
    ts(T.ij[:, :], T.is1[:, :], 15, None, A.bitwise_and)
    need("v", ip)
    for i, (sh, m) in enumerate(((0, 15), (4, 7), (4, 1), (3, 3), (5, 3), (0, 7))):
        t = ts(T.pi[:, i:i + 1], T.ip[:, 0:1], sh, m, A.arith_shift_right, A.bitwise_and)
    slots(0, 1)
    need("v", t)
    pf = copy(T.pf[:, 0:6], T.pi[:, 0:6])
    qf = T.pf[:, 0:1]
    need("s", pf)
    act(T.selw[:, 128:256], T.ones[:, :], 0.0, T.pf[:, 2:3])
    i3c = lin(cf(7), T.pf[:, 4:5], T.pf[:, 5:6], 8.0)
    qh = act(cf(12), qf, 0.0, 0.5)
    lane = lin(cf(13), qf, T.pf[:, 1:2], 8.0)
    slots(1, 2)
    need("v", pf)
    ts(grp, T.is1[:, 0:8], T.pf[:, 1:2], None, A.is_equal)
    ts(T.ind4[:, :], T.is1[:, 0:4], T.pf[:, 3:4], None, A.is_equal)
    ts(cf(17), qf, 8.0, -127.0, A.is_ge, A.mult)
    mf = ts(T.maskf[:, :], T.ij[:, :], qf, None, A.is_equal)
    slots(2, 4)
    need("v", lpl)
    loi = ts(T.loi[:, :], T.pl[:, :], 7, None, A.bitwise_and)
    lh = ts(T.lh[:, :], T.pl[:, :], 2048.0, 0.5, A.is_ge, A.mult)
    slots(4, 5)
    need("v", lh)
    lob = tt(T.lob[:, :], T.loi[:, :], T.lh[:, :], A.add)
    slots(5, 8)
    need("v", lzz)
    zh = ts(T.zh[:, :], T.zz[:, :], 3, 255, A.arith_shift_right, A.bitwise_and)
    slots(8, 9)
    need("v", zh, i3c)
    zf = copy(T.zf[:, :], T.zh[:, :])
    i3 = ts(T.i32f[:, :], T.is1[:, 0:32], cf(7), None, A.is_equal)
    wf = slots(9, 16)
    grh = copy(T.grh[:, :], grp)
    copy(T.clist[:, 0:8], T.is1[:, 0:8])
    clist = copy(T.clist[:, 8:16], T.is1[:, 1:16:2])
    need("v", il, lane)
    lt = ts(T.lt[:, :], T.il[:, :], cf(13), None, A.is_gt)
    gt = ts(T.gt[:, :], T.il[:, :], cf(13), None, A.is_lt)
    need("v", i8)
    s64 = ts(T.s64[:, :], T.i8[:, :], T.pf[:, 1:2], None, A.is_equal)
    need("g", lt)
    ma = did(g.affine_select(T.ma[:, :], T.lt[:, :], [[-1, 128]], A.not_equal, READS, 0, 1), "gi")
    need("g", gt)
    mb = did(g.affine_select(T.mb[:, :], T.gt[:, :], [[-1, 128]], A.not_equal, -READS, 0, 1), "gi")
    bwf = {s: did(g.iota(T.bw[:, B0 + 1024 * s:B0 + 1024 * s + 1024], [[0, 1024]], 1, 0,
                         allow_small_or_imprecise_dtypes=True), "gi") for s in (1, 2, 3)}

    need("s", mf)
    act(cf(0), row(R_F), 0.0, 2.0 ** -11)
    act(cf(14), row(R_E), 0.0, -1.0)
    t = act(cf(15), row(R_SLOT), 0.0, -1.0)
    act(cf(5), row(R_F), 0.0, -1023.5)
    act(cf(16), row(R_F), 0.0, -1534.0)
    act(cf(2), row(R_F), 0.0, 2.0 ** -3)
    rnd = act(cf(6), row(R_F), 0.0, ROUND)
    need("s", t)
    se = lin(T.selw[:, 0:128], T.selw[:, 128:256], 1.0, -1.0)
    lin(cf(1), row(R_SLOT), cf(14), 1.0)
    lin(cf(4), row(1), row(0), LIFT)
    t = lin(cf(8), row(R_E), cf(15), 1.0)
    act(T.r3[:, 0:8], grp, 0.0, row(0))
    need("s", zf)
    for b in range(8):
        h, bb = b // 4, b % 4
        c = 128 * h + 16 * b
        lz = act(T.lz[:, c:c + 16], T.zf[:, 16 * h:16 * h + 16], 0.0, T.ind4[:, bb:bb + 1])
    need("s", t)
    r3 = act(T.r3[:, 8:16], grp, 0.0, cf(4))
    lin(cf(9), row(R_F), cf(1), 1.0)
    t = act(cf(3), cf(1), 0.0, 256.0)
    for i, x in zip(cols, (cf(8), cf(2), cf(0), cf(3), cf(1))):
        if i == cols[3]:
            need("s", t)
        r1 = act(T.r1[:, i], grp, 0.0, x)

    for s in range(4):
        dlo = dma("y", T.lor[:, 128 * s:128 * s + 128], T.lob[32 * s:32 * s + 32, :], "dlo", lob)
    need("t", cst)
    pc = P(te.matmul(T.psa[:, 0:40], T.onef[0:1, :], T.con[0:1, :], True, False))
    need("t", dlo, e8)
    plo = P(te.matmul(T.psl[:, :], T.e8[0:8, :], T.lor[:, :], True, True))
    need("t", lz, i3)
    te.matmul(T.psb[:, 0:32], T.lz[:, 0:128], T.i32f[:, :], True, False)
    pz = P(te.matmul(T.psb[:, 0:32], T.lz[:, 128:256], T.i32f[:, :], False, True))
    need("v", plo, qh)
    selm = ts(T.selm[:, :], T.psl[:, :], cf(12), None, A.is_equal)
    need("v", pz)
    offm = copy(T.offm[:, :], T.psb[:, 0:32])

    need("s", a0, own0)
    dst = dma("y", T.c0[:, :], T.land0[:, 0:16, :], "dst", a0, own0)
    for b in range(4):
        dpb = dma("s", T.poolw[16 * b:16 * b + 16, :], T.land0[:, 16:80, :], "dpb")
        dpa = dma("y", T.poolw[16 * b + 64:16 * b + 80, :], T.land0[:, 16:80, :], "dpa")
    dwa = dma("y", T.win[R_F:128:16, :], T.land1[:, :, :], "dwa", a1, own1, wf)
    dwb = dma("s", T.win[R_E:128:16, :], T.land1[:, :, :], "dwb", a1, own1, wf)
    dwq = dma("y", T.wq[:, :], T.land1[:, :, :], "dwq")
    need("s", t)
    t = act(cf(10), cf(9), 0.0, 256.0)
    act(T.r2[:, 1:16:2], grp, 0.0, cf(9))
    pcf = lin(cf(18), qf, cf(17), 16.0)
    need("s", t, idn)
    r2 = act(T.r2[:, 0:16:2], grp, 0.0, cf(10))
    idk = act(T.idk[:, :], T.idn[:, :], 0.0, LIFT / 2048)

    gby, kept, bank = {}, {}, [None] * 4

    def gather(s):
        gby[s] = tt(T.gby[:, 128 * s:128 * s + 128], T.poolw[:, :].indirect(T.offm[:, 8 * s:8 * s + 8]),
                    T.selm[:, 128 * s:128 * s + 128], A.mult)

    def segment(i):
        need("t", gby[0], se)
        for h in (0, 128):
            p = P(te.matmul(T["ps%d" % i][:, h:h + 128], T.selw[32 * i:32 * i + 32, h:h + 128],
                            T.gby[32 * i:32 * i + 32, 0:128], True, True))
        need("s", p)
        t = B0 + 256 * i
        kept[0] = bank[i] = lin(T.bw[:, t:t + 256], T["ps%d" % i][:, 0:256], row(1), row(0))

    def thousand(s):
        a, ps = 128 * s - 128, T["ps%d" % (s - 1)][0:64, 0:128]
        need("t", gby[s], s64, bank[s - 1])
        p = P(te.matmul(ps, T.s64[:, :], T.gby[:, 128 * s:128 * s + 128], True, True))
        need("s", p)
        t = act(T.seg[0:64, a:a + 128], ps)
        kept[s] = dma("y", T.bw[0:128:16, B0 + 1024 * s:B0 + 1024 * s + 1024], T.seg[0:64, a:a + 128], "dk%d" % s, t, bwf[s])

    def letters(s, tok):
        need("s", tok, permo)
        return act(T.outs[:, 128 * s:128 * s + 128], T.ent[:, 128 * s:128 * s + 128].indirect(T.permo[:, :]))

    def spread(out, tile):
        return tt(out[:, :], tile[:, :].indirect(T.clist[:, 0:8]), T.maskf[:, :], A.mult)

    need("v", dst)
    sl = ts(T.sl[:, :], T.c0[:, :], 2047, None, A.bitwise_and)
    h0 = ts(T.h0[:, :], T.c0[:, :], 2.0 ** -11, -0.499755859375, A.mult, A.add)
    need("v", sl)
    off = copy(T.off[:, 0:8], T.sl[:, :])
    need("v", h0, clist)
    t = spread(T.sph, T.h0)
    need("t", t, grh)
    ph = P(te.matmul(T.psc[:, 0:8], T.sph[:, :], T.grh[:, :], True, True))
    need("v", dpa, dpb, offm, selm)
    gather(0)
    segment(0)

    W, WB = T.w[:, 16:144:16], T.w[:, 0:128:16]
    Y = T.y[:, 1:16:2]
    for s in range(4):
        c = 8 * s
        E, look = T.ent[:, 128 * s:128 * s + 128], T.win[:, :].indirect(T.off[:, c:c + 8])
        if s == 0:
            need("v", off, rnd, dwa, dwb)
            ent = ts(E, look, cf(5), cf(6), A.add, A.add)
            need("t", pc, ent, r1)
            pe = P(te.matmul(T.psa[:, 0:40], E, T.r1[:, :], False, True))
            dlw = dma("y", T.win[R_SYM:128:16, :], T.land3[:, :, :], "dlw", a3, own3, ent)
            for i in (1, 2, 3):
                segment(i)
            need("v", ph)
            for i in (0, 1):
                h2 = ts(T.h2[:, i:16:2], T.psc[:, 0:8], 2048.0, None, A.add)
            need("v", dwq)
            t = ts(T.tb[:, 0:128], T.wq[:, :], 2.0 ** -11, 0.500244140625, A.mult, A.add)
            dma("y", T.win[R_F:128:16, :], T.tb[:, 0:128], "dtb", t)
            t = ts(T.tb[:, 128:256], T.wq[:, :], 2047, None, A.bitwise_and)
            dtb = dma("y", T.win[R_E:128:16, :], T.tb[:, 128:256], "dtb", t)
            need("v", pe, h2)
            pr = tt(T.pr[:, :], T.psa[:, 8:24], T.h2[:, :], A.mult)
            need("v", pcf)
            permo = ts(T.permo[:, :], T.is1[:, 0:8], 2.0, cf(18), A.mult, A.add)
            need("v", pr)
            w = tt(W, T.pr[:, 1:16:2], T.psa[:, 0:8], A.is_lt)
            xq = tt(T.xq[:, :], T.pr[:, :], T.psa[:, 24:40], A.add)
            need("v", xq)
            X = T.xq[:, :]
        else:
            need("t", wc)
            te.matmul(T.psb[:, 0:8], T.ones[:, :], T.wc[:, 2 * c - 9:2 * c - 1], True, False)
            need("v", off, dlw, dtb, hr)
            ent = tt(E, look, T.hr[:, :], A.mult)
            need("t", ent, r2)
            pe = P(te.matmul(T.psa[:, 0:16], E, T.r2[:, 0:16], True, True))
            sym = letters(s, ent)
            if s < 3:
                gather(s + 1)
                thousand(s + 1)
            else:
                sym = letters(0, copy(T.ent[:, 0:128], T.win[:, :].indirect(T.off[:, 0:8])))
            need("v", pe)
            w = ts(W, T.psa[:, 1:16:2], 4096.0, None, A.is_lt)
            X = T.psa[:, 0:16]
        y = scan(T.y[:, :], T.lift[:, :], X, 0.0, A.add, A.min)
        need("t", w, ma, mb)
        te.matmul(T.psb[:, 0:8], T.ma[:, :], W, s == 0, False)
        cn = P(te.matmul(T.psb[:, 0:8], T.mb[:, :], WB, False, True))
        need("v", y)
        if s < 3:
            ylo = ts(T.ylo[:, :], Y, 2047, None, A.bitwise_and)
            hx = ts(T.hx[:, R_F:128:16], Y, 2.0 ** -11, 1533.500244140625, A.mult, A.add)
            need("t", idk, selm)
            te.matmul(T.psl[:, 0:128], T.w[:, 16:144], T.idk[:, :], True, False)
            need("t", hx, idn)
            pr_ = P(te.matmul(T.psl[:, 0:128], T.hx[:, :], T.idn[:, :], False, True))
        else:
            t = tt(T.spf[:, :], T.y[:, :].indirect(T.clist[:, 8:16]), T.maskf[:, :], A.mult)
        need("v", cn)
        off2 = scan(T.off2[:, c:c + 8], T.psb[:, 0:8], WB, B0 - READS, A.add, A.add)
        need("s", off2, con, kept[s])
        gb = act(T.gb[:, :], T.bw[:, 0:B0 + 1024 + 1024 * s].indirect(T.off2[:, c:c + 8]))
        if s < 3:
            need("v", ylo)
            t = spread(T.sph, T.ylo)
            wc = scan(T.wc[:, 2 * c:2 * c + 8], W, T.zer[:, :], T.wc[:, 2 * c - 9:2 * c - 8] if s else 0.0, A.add, A.add)
            need("t", t)
            te.matmul(T.psc[:, 0:8], T.sph[:, :], T.grh[:, :], True, False)
        else:
            need("t", t)
            te.matmul(T.psc[:, 0:8], T.spf[:, :], grp, True, False)
        need("t", gb, r3)
        pb = P(te.matmul(T.psc[:, 0:8], T.gb[:, :], T.r3[:, 0:8] if s < 3 else T.r3[:, 8:16], False, True))
        if s == 0:
            gather(1)
        need("v", pb)
        if s == 3:
            xl = copy(T.xl[:, :], T.psc[:, 0:8])
            break
        off = copy(T.off[:, c + 8:c + 16], T.psc[:, 0:8])
        need("s", pr_)
        hr = lin(T.hr[:, :], T.psl[:, 0:128], cf(16), 1.0 / READS)
        if s == 0:
            thousand(1)

    dsy = dma("y", T.snd4[:, :, :], T.outs[R_SYM:128:16, :], "dsy", sym)
    dow4 = dma("y", T.land4[me, :, :], T.outs[16 * me + R_SYM:16 * me + R_SYM + 1, :], "dow4")
    need("g", dsy)
    a4 = send(T.snd4, T.land4, "a4")
    dla = dma("y", T.snd5[:, :, :], T.xl[:, :], "dla", xl)
    dow5 = dma("y", T.land5[me, :, :], T.xl[16 * me:16 * me + 16, :], "dow5")
    need("g", dla)
    a5 = send(T.snd5, T.land5, "a5")
    dma("s", T.syms[:, :], T.land4[:, :, :], "fsy", a4, dow4)
    dma("y", T.last[:, :], T.land5[:, :, :], "fla", a5, dow5)
    for sem in sorted(cnt):
        if waited.get(sem, 0) < cnt[sem]:
            need("g", (sem, cnt[sem]))
